import numpy as np, ml_dtypes
CORES = [1,5,17,21,33,37,49,53]
N = 8
import mx_ref
BF = ml_dtypes.bfloat16
def entries(a):
    return np.ascontiguousarray(a.T).reshape(-1)
def table(e):
    return np.ascontiguousarray(np.reshape(e, (-1, 16)).T).astype(np.int32)
def cols(t, e):
    v = np.concatenate([t.reshape(128, -1, 4), np.zeros((128, 1, 4), BF)], axis=1)
    return np.ascontiguousarray(v[:, e]).reshape(128, -1)
def cut(t, i, w=512):
    return t[:, w * i:w * i + w]
def f(rng, *shape):
    return mx_ref.flush((rng.standard_normal(shape, dtype=np.float32) * np.exp2(rng.integers(-2, 3, shape[:-1] + (1,)))).astype(BF))
def wide(rng, *shape, cols=0):
    v = rng.standard_normal(shape, dtype=np.float32) * np.exp2(rng.integers(-12, 13, shape)).astype(np.float32)
    if cols: v *= np.repeat(np.exp2(rng.integers(-cols, cols + 1, shape[:-2] + (1, shape[-1] // 4))) * (rng.random(shape[:-2] + (1, shape[-1] // 4)) > 0.0625), 4, axis=-1).astype(np.float32)
    return mx_ref.flush(v.astype(BF))
C, P, B, O, DN, DS = 192, 384, 3, 2, 224, 112
def lists(rng, S, straddle=0.5, fill="any", flip=None):
    o = np.array([[max(0, min(S[r + 1], P * q + P) - max(S[r], P * q)) for q in range(N)] for r in range(N)])
    ends, both = np.zeros((N, N), int), {}
    for r in range(N):
        for q in range(N - 1):
            if o[r, q] > 0 and o[r, q + 1] > 0 and rng.random() < straddle:
                a = int(rng.integers(1, min(5, o[r, q]) + 1))
                b = int(rng.integers(1, min(6 - a, o[r, q + 1]) + 1))
                if fill == "few":
                    a = int(o[r, q] % 6); b = 6 - a
                    if a == 0: continue
                o[r, q] -= a; o[r, q + 1] -= b
                ends[r, q] += 1; ends[r, q + 1] += 1; both[r, q] = a + b
    K = np.floor_divide(o + 5, 6)
    segs = [(r, q) for r in range(N) for q in range(N) if o[r, q] > 0]
    segs = [segs[i] for i in rng.permutation(len(segs))]
    if fill == "full": segs = [s for s in segs if s[1] % 2 == 1] + [s for s in segs if s[1] % 2 == 0]
    if fill == "few": segs = []
    for r, q in segs:
        room = int(min(DS - ends[r, q] - K[r, q], o[r, q] - K[r, q], C - (ends[r].sum() >> 1) - K[r].sum(), DN - ends[:, q].sum() - K[:, q].sum()))
        K[r, q] += room if fill == "full" else rng.integers(0, room + 1)
    m = np.zeros((N, C), int)
    for r in range(N):
        e = []
        for q in range(N):
            k = int(K[r, q])
            e += (1 + np.bincount(rng.permutation(np.repeat(np.arange(k), 5))[:o[r, q] - k], minlength=k)).tolist()
            if (r, q) in both: e.append(both[r, q])
        m[r, np.sort(rng.permutation(C)[:len(e)])] = np.array(e, int)
    if flip is None: flip = rng.random() < 0.5
    if flip: m = m[::-1, ::-1]
    return {"cnt": np.stack([table(e) for e in m])}
def begins(rng):
    for k in range(50):
        S, e = [0], 1 - 2 * int(rng.integers(2))
        turn = N if rng.random() < 0.5 else int(rng.integers(2, N))
        for r in range(1, N):
            if r == turn: e = -e
            s = S[-1] - P * (r - 1)
            lo = max(s - P, -2 * P, -((3 * P * (N - r)) >> 1))
            hi = min(s + ((3 * P) >> 1), 2 * P, P * (N - r))
            a, b = (max(lo, (3 * P) >> 2), hi) if e > 0 else (lo, min(hi, -((3 * P) >> 2)))
            if a > b: a = b = hi if e > 0 else lo
            S.append(P * r + int(rng.integers(a, b + 1)))
        S.append(N * P)
        own = sum(max(0, min(S[r + 1], P * r + P) - max(S[r], P * r)) for r in range(N))
        if 2 * own <= N * P: return S
    raise RuntimeError("begins")
def floats(rng):
    return {"x": f(rng, N, 128, 4 * C), "w": f(rng, N, 128, 512 * B * O)}
def setup_inputs(rng):
    return {**floats(rng), **lists(rng, begins(rng))}
def setup_inputs_full(rng):
    S = [0] + [P * r + (P >> 1) + int(rng.integers(-(P >> 4), (P >> 4) + 1)) for r in range(1, N)] + [N * P]
    return {**floats(rng), **lists(rng, S, straddle=2.0, fill="full")}
def setup_inputs_furthest(rng):
    S = [0] + [min(P * (r + 2), N * P) for r in range(1, N + 1)]
    return {**floats(rng), **lists(rng, S, straddle=2.0, fill="few")}
def setup_inputs_dense(rng):
    def some(k, n):
        return (1 + np.bincount(rng.permutation(np.repeat(np.arange(k), 5))[:n - k], minlength=k)).tolist()
    H = min(P // 256 * 128 + 64, P - DS) if N > 4 else (P - 1) // 256 * 128 + 64
    X = (7 * DS - P) // 5
    flip = bool(rng.random() < 0.5)
    front = 3 + 2 * int(rng.integers((N - 2) // 2))
    e = [[] for r in range(N)]
    for q in range(2, N):
        h, i, j = P // 2, 0, 0
        if q == front: h, i, j = (P - DS, X, DS) if flip else (DS, DS, X)
        elif q % 2 == 1 or N == 4: h, i, j = H, H % 128, 128 - H % 128
        a, b = h - i, P - h - j
        if q == 2: a += 2 * P
        if q % 2 == 1: ka, kb = DS - i, DS - j
        else:
            ka = int(rng.integers(-(-a // 6), (C if q == 2 else C - DS) - i + 1))
            kb = int(rng.integers(-(-b // 6), C - DS - j + 1))
        e[q - 2] += some(ka, a) + [1] * i
        e[q - 1] += [1] * j + some(kb, b)
    m = np.zeros((N, C), int)
    for r in range(N):
        m[r, np.sort(rng.permutation(C)[:len(e[r])])] = np.array(e[r], int)
    if flip: m = m[::-1, ::-1]
    return {**floats(rng), "cnt": np.stack([table(v) for v in m])}
def setup_inputs_many(rng):
    def some(k, n):
        return (1 + np.bincount(rng.permutation(np.repeat(np.arange(k), 5))[:n - k], minlength=k)).tolist()
    src = [[0], [0, 1, 2, 3], [3], [3]] if N == 4 else [[0], [0], [0, 1, 2, 3, 4], [4], [4], [4, 5, 6, 7], [7], [7]]
    flip = bool(rng.random() < 0.5)
    lo = -(-P // 6)
    alone = [src.count([r]) for r in range(N)]
    among = [sum(len(s) > 1 and r in s for s in src) for r in range(N)]
    least = [alone[r] * lo + (1 - among[r] - alone[r] * lo) % N for r in range(N)]
    k = np.zeros((N, N), int)
    for q, s in enumerate(src):
        if len(s) == 1: continue
        c = np.ones(len(s), int)
        c[int(rng.integers(1, len(s) - 1))] = N - len(s) + 1
        top = np.array([(min(DS, (C - least[r]) // among[r]) - int(c[i])) // N for i, r in enumerate(s)])
        j = np.ones(len(s), int)
        while j.sum() < DN // N - 1: j[int(rng.choice(np.flatnonzero(j < top)))] += 1
        k[s, q] = N * j + c
    for r in range(N):
        n = alone[r]
        if n == 0: continue
        z = min(C - int(k[r].sum()), n * DS)
        w = least[r] + N * int(rng.integers(0, (z - least[r]) // N + 1))
        for q in range(N):
            if src[q] == [r]:
                n -= 1
                u = int(rng.integers(max(lo, w - DS * n), min(DS, w - lo * n) + 1))
                k[r, q] = u; w -= u
    e = [[] for r in range(N)]
    for q, s in enumerate(src):
        v = some(int(k[:, q].sum()), P)
        for r in s:
            i = int(k[r, q])
            e[r] += v[:i]; v = v[i:]
    m = np.zeros((N, C), int)
    for r in range(N):
        m[r, np.sort(rng.permutation(C)[:len(e[r])])] = np.array(e[r], int)
    if flip: m = m[::-1, ::-1]
    return {**floats(rng), "cnt": np.stack([table(v) for v in m])}
def setup_inputs_spread(rng):
    d = setup_inputs(rng); v = np.array(wide(rng, N, 128, 4 * C, cols=6))
    v[np.abs(v.astype(np.float32)) < 2.0 ** -30] = 0
    d["x"] = v; return d
def check_inputs(d):
    b = []
    for k in ("x", "w"):
        v = np.abs(d[k].astype(np.float32))
        if not ((v == 0) | ((v >= 2.0 ** -30) & (v <= 2.0 ** 30))).all(): b.append("the range of " + k)
    m = np.stack([entries(a) for a in d["cnt"]])
    if m.min() < 0 or m.max() > 6: return b + ["cnt"]
    if m.sum() != N * P: return b + ["the sum of all counts"]
    runs = np.repeat(np.arange(N * C), m.reshape(-1)).reshape(N, P)
    for q in range(N):
        u = np.unique(runs[q])
        k = np.bincount(np.floor_divide(u, C), minlength=N)
        if len(u) > DN: b.append("different columns in a run")
        if k.max() > DS: b.append("different columns of one rank in a run")
        if (np.abs(np.flatnonzero(k) - q) > 2).any(): b.append("a column of a rank more than two away")
    return b
def reference(x, w, cnt):
    m = np.stack([entries(a) for a in cnt])
    runs = np.repeat(np.arange(N * C), m.reshape(-1)).reshape(N, P)
    t = np.concatenate([x[r] for r in range(N)], axis=1)
    y = np.zeros((N, 128, O * P), np.float32)
    for q in range(N):
        for b in range(B):
            c = mx_ref.quantize(cols(t, runs[q, 128 * b:128 * b + 128]))
            for o in range(O):
                i = P * o + 128 * b
                y[q][:, i:i + 128] = mx_ref.matmul(mx_ref.quantize(cut(w[q], O * b + o)), c)
    return {"y": y}

@@ -1,0 +1,360 @@
+from concourse.bass import DstId, RemoteDMATransfer
+from concourse.mybir import dt, AluOpType as Op, AxisListType, ActivationFunctionType as Act
+
+C, P, NB, NO, H = 192, 384, 3, 2, 112
+W0 = 1536
+TR = 3584
+FAR = 4096
+BIG = 1.0e6
+WIN = 3 * H + 2 * C
+F32, I32, U16, U8, F8, BF = "float32", "int32", "uint16", "uint8", "float8_e4m3fn_x4", "bfloat16"
+
+
+def sb(n, t):
+    return ("sbuf", [128, n], t)
+
+
+SCRATCH = {
+    "xt": sb(4 * C, BF), "wt": sb(512 * 6, BF), "wq": sb(768, F8), "ws": sb(768, U8),
+    "raw": sb(C, F8), "raws": sb(C, U8), "comp": sb(C, F8), "comps": sb(C, U8),
+    "sel2": sb(H, F8), "sel2s": sb(H, U8), "selz": sb(H, F8), "selzs": sb(H, U8),
+    "win": sb(WIN, F8), "wins": sb(WIN, U8), "fin": sb(P, F8), "fins": sb(P, U8),
+    "pi": sb(1, I32), "pa": sb(1, I32), "pf": sb(1, F32), "c16": sb(16, F32), "tj": sb(16, F32), "tji": sb(26, I32),
+    "tjj": sb(26, I32), "m2": sb(16, F32), "ir": sb(C, F32), "op": sb(2 * C, F32), "vz": sb(2 * H, F32), "zi": sb(H, F32),
+    "mi": sb(16, I32), "mj": sb(16, I32), "mask": sb(P, F32), "rm": sb(64, BF), "rs": sb(26, F32),
+    "tb": sb(12, I32), "row1": sb(C, BF), "row": sb(C, BF), "T1": sb(64, BF), "A1": sb(96, BF), "B1": sb(64, BF),
+    "Z1": sb(64, BF), "ee": sb(27, F32), "uu": sb(26, F32), "z0": sb(26, F32), "zz": sb(26, F32),
+    "sx": sb(26, F32), "su": sb(26, U16), "kr": sb(11776, F32), "kd": sb(C, F32), "kl": sb(12, U16), "ke": sb(12, U16),
+    "er": sb(2 * C, F32), "sc": sb(C, F32),
+    "f2": sb(1, F32), "l2": sb(8, U16), "r2": sb(H, F32), "d0": sb(H, F32), "d2": sb(H, F32), "dz": sb(H, F32),
+    "t0": sb(8, U16), "t2": sb(8, U16), "tz": sb(8, U16), "rz": sb(H, F32),
+    "tl": sb(12, F32), "S": sb(1, F32), "pc": sb(1, F32), "jk": sb(C, F32), "js": sb(8, F32), "acc": sb(1, F32),
+    "lze": sb(8, U16), "pt": sb(12, U16), "po": sb(24, U16), "ct": sb(16, U16), "cz": sb(8, U16),
+    "pw": sb(14336, F32), "pm": sb(P + 16, F32), "pd": sb(P, F32), "il": sb(24, U16),
+    "ysb": sb(NO * P, F32), "ps": ("psum", [128, 512 * 6], F32),
+}
+SEMAPHORES = ["sv", "sa", "sg", "st", "dtab", "drow", "dx", "dw0", "dw1", "down", "dy", "sent",
+              "atot", "apt", "apc", "act", "acz", "acd"]
+
+
+def common(topo, src, dsts):
+    e = topo.engines(src, dsts[0])
+    for d in dsts[1:]:
+        e = [k for k in e if k in topo.engines(src, d)]
+    return e
+
+
+def bits(e):
+    m = 0
+    for k in e:
+        m |= 1 << k
+    return m
+
+
+def rank_program(g, core, T, topo):
+    r = T.rank_of(core)
+    if r is None:
+        return
+    cores = T.cores
+    N = len(cores)
+    half = N // 2
+
+    def partner(q):
+        return [d for d in (q - 1, q + 1) if 0 <= d < N and topo.chip(cores[d]) == topo.chip(cores[q])][0]
+
+    def two(q):
+        return [d for d in (q - 2, q + 2) if 0 <= d < N]
+
+    def zed(q):
+        return [d for d in (q - 1, q + 1) if 0 <= d < N and d != partner(q)]
+
+    def seg(d):
+        a, o = {}, 0
+        for s in range(max(0, d - 2), min(N, d + 3)):
+            n = C if s in (d, partner(d)) else H
+            a[s] = (o, n)
+            o += n
+        return a
+
+    def eng(q):
+        return common(topo, cores[q], [c for c in cores if c != cores[q]])
+
+    def inner(q):
+        return [e for e in topo.engines(cores[q], cores[partner(q)]) if e not in eng(q)] or eng(q)
+
+    def share(q, d):
+        e, v = eng(q), two(q)
+        n = len(e) // len(v)
+        return e[n * v.index(d):n * v.index(d) + n]
+
+    def summed(d):
+        return list(range(d)) if d < half else list(range(d + 1, N))
+
+    def slot(s, d):
+        if s in summed(d):
+            return half - len(summed(d)) + summed(d).index(s)
+        return 2 * half if s == partner(d) and s < d else None
+
+    pt, me, E = partner(r), seg(r), eng(r)
+    lo2 = r - 2 if r - 2 >= 0 else None
+    hi2 = r + 2 if r + 2 < N else None
+    z = (zed(r) + [None])[0]
+    tr = float(TR * (1 + (r + r // half) % 2))
+    qs = {"v": g.vector, "a": g.scalar, "s": g.sync, "t": g.tensor, "g": g}
+    home = {"v": "sv", "a": "sa", "t": "st", "g": "sg"}
+    seen, total = {}, {}
+
+    def need(q, toks):
+        for sem, val in toks:
+            if seen.get((q, sem), 0) < val:
+                qs[q].wait_ge(T.sem[sem], val)
+                seen[(q, sem)] = val
+
+    def do(q, deps, fn, sem=None, n=1):
+        need(q, deps)
+        s = sem or home[q]
+        fn().then_inc(T.sem[s], n)
+        total[s] = total.get(s, 0) + n
+        return (s, total[s])
+
+    V, A = g.vector, g.scalar
+
+    def dma(q, sem, out, in_, deps=()):
+        return do(q, deps, lambda: qs[q].dma_start(out, in_), sem, 16)
+
+    def dst(c):
+        rid, pid, _ = topo.addr(c)
+        return DstId(rid=rid, pnc=pid)
+
+    sent = [0]
+
+    def fused(deps, trs):
+        need("g", deps)
+        g.remote_dma_fused([RemoteDMATransfer(dst_ids=[dst(cores[d]) for d in ds], dma_engine_mask=bits(e), remote_sem=T.sem[sem],
+                                              srcs=[a], dsts=b) for ds, e, sem, a, b in trs], local_sem=T.sem.sent)
+        sent[0] += sum(len(e) for ds, e, sem, a, b in trs)
+
+    def tc(deps, out, in_):
+        return do("v", deps, lambda: V.tensor_copy(out, in_))
+
+    def tt(deps, out, a, b, op):
+        return do("v", deps, lambda: V.tensor_tensor(out, a, b, op))
+
+    def ts(deps, out, a, s1, op0, s2=None, op1=None):
+        if op1 is None:
+            return do("v", deps, lambda: V.tensor_scalar(out, a, s1, None, op0))
+        return do("v", deps, lambda: V.tensor_scalar(out, a, s1, s2, op0, op1))
+
+    def scan(deps, out, a, b, init, op0, op1):
+        return do("v", deps, lambda: V.tensor_tensor_scan(out, a, b, init, op0, op1))
+
+    def diag(deps, out, row, n):
+        return scan(deps, out, T.mask[:, 0:n], row, 0.0, Op.max, Op.min)
+
+    def fill(ap, c):
+        return do("v", (), lambda: V.memset(ap, c))
+
+    def act(deps, out, in_, func=Act.Copy, **kw):
+        return do("a", deps, lambda: A.activation(out, in_, func, **kw))
+
+    def pick(deps, out, in_, o):
+        return tc(deps, out.bitcast(dt.uint32), in_.bitcast(dt.uint32).indirect(o))
+
+    def quant(i, j, d):
+        return do("v", [d], lambda: V.quantize_mx(T.wq[:, i:j], T.ws[:, i:j], T.wt[:, 4 * i:4 * j]))
+
+    def codes(ap):
+        return ap.bitcast(dt.uint8)
+
+    shift = -P * z - 0.5 if z is not None else 0.0
+
+    def base(d):
+        return float(W0 - P * d) - shift
+
+    for k in range(8):
+        dtab = dma("s" if k % 2 == 0 else "a", "dtab", T.tb[16 * k:16 * k + 16, :], T.cnt[:])
+    dx = dma("a", "dx", T.xt[:], T.x[:])
+
+    flag = {"allow_small_or_imprecise_dtypes": True}
+    k4 = do("g", (), lambda: g.iota(T.mi[:], [[1, 16]], 0, 15))
+    k1 = do("g", (), lambda: g.iota(T.c16[:], [[16, 16]], 0, 0, **flag))
+    k0 = do("g", (), lambda: g.iota(T.pi[:], [[0, 1]], 0, 1))
+    k5 = do("g", (), lambda: g.iota(T.tji[:], [[128, 26]], FAR * (1 + r % 2), 1))
+    k3 = do("g", (), lambda: g.iota(T.ir[:, 0:C], [[1, C]], 0, 0, **flag))
+    ft = fill(T.T1[:], 0.0)
+    u = fill(T.rm[:], 1.0)
+    v = ts([k4], T.mj[:], T.mi[:], 15, Op.bitwise_and)
+    fill(T.A1[:, 31:32], 0.0)
+    mk = ts([v], T.mask[:, 0:16], T.mj[:], 0.0, Op.is_equal, BIG, Op.mult)
+    fr = do("v", [u], lambda: V.memset(T.rm[:, 0:32:16], 0.0))
+    u = ts([k0], T.pa[:], T.pi[:], 15, Op.bitwise_and)
+    jj = ts([k5], T.tjj[:], T.tji[:], 16383 - 127 + 15, Op.bitwise_and)
+    pf = tc([u], T.pf[:], T.pa[:])
+
+    def const(deps, out, c):
+        return act([k1] + list(deps), out, T.c16[:, 0:1], Act.Identity, scale=0.0, bias=float(c))
+
+    fs = const((), T.tl[:, half:half + 1], shift if r < half else -(N * P + shift))
+    e0 = const((), T.er[:, 0:1], 0)
+    fz = const((), T.ee[:, 0:1], 0)
+    act([k1], T.rs[:, 0:13], T.c16[:, 0:13], Act.Identity, scale=0.0, bias=1.0)
+    act([k1], T.rs[:, 14:26], T.c16[:, 0:12], Act.Identity, scale=0.0, bias=1.0)
+    fz = const((), T.rs[:, 13:14], 0)
+    n = 16
+    while n < P:
+        w = min(n, P - n)
+        mk = act([mk], T.mask[:, n:n + w], T.mask[:, 0:w])
+        n += w
+        if n == 32:
+            j0 = act([pf], T.tj[:], T.c16[:], Act.Identity, bias=T.pf[:])
+        if n == 64:
+            kr = act([k3], T.kr[:, 0:C], T.ir[:, 0:C], Act.Identity, bias=float(C))
+            j3 = act([j0], T.m2[:], T.tj[:], Act.Identity, scale=-2.0, bias=-float(C - H))
+        if n == 256:
+            ep = act([k3], T.er[:, C:2 * C], T.ir[:, 0:C], Act.Identity, bias=tr)
+
+    a0 = tc([dtab, ft], T.T1[:, 0:12], T.tb[:])
+    a1 = ts([dtab], T.T1[:, 14:26], T.tb[:], 0.0, Op.is_gt)
+    b1 = do("v", [a1, fr], lambda: V.transpose(T.A1[:, 32:96], T.T1[:]))
+    drow = dma("s", "drow", T.row1[0:1, :], T.A1[0:12, 32:48], [b1])
+    dw0 = dma("s", "dw0", T.wt[:, 0:1536], T.w[:, 0:1536])
+    dw1 = dma("s", "dw1", T.wt[:, 1536:3072], T.w[:, 1536:3072])
+    z0 = ts([a1], T.z0[:], T.T1[:, 0:26], 0.0, Op.is_equal)
+    b2 = scan([b1], T.B1[:], T.A1[:, 31:95], T.rm[:], 0.0, Op.add, Op.mult)
+    zz = tt([z0, jj], T.zz[:], T.z0[:], T.tjj[:], Op.mult)
+    b3 = do("v", [b2], lambda: V.transpose(T.Z1[:], T.B1[:]))
+    ee = scan([b3, fz], T.ee[:, 1:27], T.rs[:], T.Z1[:, 32:58], 0.0, Op.mult, Op.add)
+    uu = tt([b3, zz], T.uu[:], T.Z1[:, 0:26], T.zz[:], Op.add)
+    to = [d for d in range(N) if d != r and slot(r, d) is not None]
+    if to:
+        fused([ee], [(to, E, "atot", T.ee[:, 12:13], [T.tl[:, slot(r, d):slot(r, d) + 1] for d in to])])
+    sx = tt([uu, ee], T.sx[:], T.uu[:], T.ee[:, 0:26], Op.add)
+    f2 = act([ee], T.f2[:], T.ee[:, 26:27], Act.Relu, bias=-float(H))
+    if r >= half:
+        fs = act([ee], T.tl[:, half + 1:half + 2], T.ee[:, 12:13])
+    act([mk], T.pw[:, W0 - 16:W0 + P - 16], T.mask[:, 0:P], scale=0.0)
+    fp = act([mk], T.pw[:, W0 + P - 16:W0 + P], T.mask[:, 0:16], scale=0.0)
+    for k, s in enumerate((r, pt)):
+        op = act([k3], T.op[:, C * k:C * k + C], T.ir[:], Act.Identity, bias=float(me[s][0]))
+    for k, s in enumerate(two(r)):
+        vz = act([k3], T.vz[:, H * k:H * k + H], T.ir[:, 0:H], Act.Identity, bias=float(me[s][0]))
+    if z is not None:
+        zi = act([k3], T.zi[:], T.ir[:, 0:H], Act.Identity, bias=float(me[z][0]))
+    sxu = tc([sx], T.su[:], T.sx[:])
+    ks = tc([sxu, kr], T.kr[:].indirect(T.su[:, 14:26]), T.ir[:, 0:C])
+    if hi2 is not None:
+        l2 = ts([f2, j0], T.l2[:, 0:7], T.tj[:, 0:7], T.f2[:], Op.add)
+    kd = diag([ks, mk], T.kd[:], T.kr[:, 0:C], C)
+    qx = do("v", [dx], lambda: V.quantize_mx(T.raw[:, 0:C], T.raws[:, 0:C], T.xt[:, 0:4 * C]))
+
+    ma, pa = me[r][0], seg(pt)[r][0]
+    pb = do("g", [drow], lambda: g.partition_broadcast(T.row[:], T.row1[0:1, :], 128))
+    fused([sxu], [([pt], E, "apt", T.su[:, 0:12], [T.pt[:]])])
+    dma("s", "down", codes(T.win[:, ma:ma + C]), codes(T.raw[:, 0:C]), [qx])
+    down = dma("s", "down", T.wins[:, ma:ma + C], T.raws[:, 0:C], [qx])
+
+    kl = ts([kd], T.kl[:], T.kd[:, 15:C:16], C - 1.0, Op.min)
+    ke = tc([kd], T.ke[:], T.kd[:, 15:C:16])
+    er = scan([pb], T.er[:, 1:C], T.row[:, 0:C - 1], T.row[:, 0:C - 1], 0.0, Op.add, Op.max)
+    cq = pick([kl, qx], T.comp[:, 0:C], T.raw[:, 0:C], T.kl[:, 0:12])
+    cs = act([kl, qx], T.comps[:, 0:C], T.raws[:, 0:C].indirect(T.kl[:, 0:12]))
+    sc = act([er, e0, ep, ke], T.sc[:, 0:C], T.er[:, 0:2 * C].indirect(T.ke[:, 0:12]))
+    src, scl, tabs, tk = {}, {}, {}, {}
+    if hi2 is not None:
+        q2 = pick([l2, cq], T.sel2[:, 0:H], T.comp[:, 0:C], T.l2[:, 0:7])
+        src[hi2] = (T.sel2, q2)
+        r2 = act([sc, l2], T.r2[:], T.sc[:, 0:C].indirect(T.l2[:, 0:7]))
+    if lo2 is not None:
+        src[lo2] = (T.comp, cq)
+    at = {d: seg(d)[r][0] for d in seg(r)}
+    fused([src[d][1] for d in two(r)], [([d], share(r, d), "acd", codes(src[d][0][:, 0:H]), [codes(T.win[:, at[d]:at[d] + H])]) for d in two(r)])
+    fused([qx], [([pt], inner(r), "apc", codes(T.raw[:, 0:C]), [codes(T.win[:, pa:pa + C])])])
+    fused([qx], [([pt], inner(r), "apc", T.raws[:, 0:C], [T.wins[:, pa:pa + C]])])
+
+    na = sum(len(eng(s)) for s in range(N) if s != r and slot(s, r) is not None)
+    a, b = half - len(summed(r)), half + 1 if r < half else half + 2
+    tS = act([fs] + ([("atot", na)] if na else []), T.js[:, 0:b - a], T.tl[:, a:b], scale=1.0 if r < half else -1.0, accum_out=T.S[:])
+    if z is not None:
+        ac = act([tS, sc], T.jk[:, 0:C - H], T.sc[:, 1:C - H + 1], Act.Sign, bias=T.S[:], accum_out=T.acc[:])
+    if pt > r:
+        pc = act([tS, ee], T.pc[:], T.ee[:, 12:13], Act.Identity, bias=T.S[:])
+    else:
+        pc = act([tS], T.pc[:], T.tl[:, slot(pt, r):slot(pt, r) + 1], Act.Identity, scale=-1.0, bias=T.S[:])
+    if lo2 is not None:
+        tabs[lo2] = (T.t0, T.d0, diag([sc], T.d0[:], T.sc[:, 0:H], H))
+    if hi2 is not None:
+        tabs[hi2] = (T.t2, T.d2, diag([r2], T.d2[:], T.r2[:], H))
+    qw = [quant(0, 384, dw0), quant(384, 768, dw1)]
+
+    if z is not None:
+        le = ts([ac, j3], T.lze[:, 0:7], T.m2[:, 0:7], T.acc[:], Op.add, -0.5, Op.mult)
+        rz = act([le], T.rz[:], T.sc[:, 0:C].indirect(T.lze[:, 0:7]))
+    if lo2 is not None:
+        scl[lo2] = (T.comps, cs)
+    if hi2 is not None:
+        scl[hi2] = (T.sel2s, act([l2, cs], T.sel2s[:, 0:H], T.comps[:, 0:C].indirect(T.l2[:, 0:7])))
+    if z is not None:
+        qzs = act([le, cs], T.selzs[:, 0:H], T.comps[:, 0:C].indirect(T.lze[:, 0:7]))
+    for d in tabs:
+        t, dd, tok = tabs[d]
+        tk[d] = ts([tok, tS], t[:, 0:7], dd[:, 15:H:16], T.S[:], Op.add, base(d), Op.add)
+    fused([tk[d] for d in two(r)], [([d], share(r, d), "act", tabs[d][0][:, 0:7], [T.ct[:, 7 * two(d).index(r):7 * two(d).index(r) + 7]]) for d in two(r)])
+    if z is not None:
+        qz = pick([le, cq], T.selz[:, 0:H], T.comp[:, 0:C], T.lze[:, 0:7])
+        u = diag([rz], T.dz[:], T.rz[:], H)
+    oo = ts([tS, sx], T.po[:, 0:12], T.sx[:, 0:12], T.S[:], Op.add, base(r), Op.add)
+    if z is not None:
+        tz = ts([u], T.tz[:, 0:7], T.dz[:, 15:H:16], T.S[:], Op.add, base(z), Op.add)
+        fused([tz], [([z], E, "acz", T.tz[:, 0:7], [T.cz[:, 0:7]])])
+        fused([qz], [([z], E, "acd", codes(T.selz[:, 0:H]), [codes(T.win[:, at[z]:at[z] + H])])])
+    fused([scl[d][1] for d in two(r)], [([d], share(r, d), "acd", scl[d][0][:, 0:H], [T.wins[:, at[d]:at[d] + H]]) for d in two(r)])
+    if z is not None:
+        fused([qzs], [([z], E, "acd", T.selzs[:, 0:H], [T.wins[:, at[z]:at[z] + H]])])
+
+    po = ts([pc, ("apt", len(eng(pt)))], T.po[:, 12:24], T.pt[:], T.pc[:], Op.add, base(r), Op.add)
+    pp = tc([oo, po, fp, op], T.pw[:].indirect(T.po[:, 0:24]), T.op[:])
+    nt = len(two(r))
+    pp = tc([pp, vz, ("act", sum(len(share(s, r)) for s in two(r)))], T.pw[:].indirect(T.ct[:, 0:7 * nt]), T.vz[:, 0:H * nt])
+    if z is not None:
+        pp = tc([pp, zi, ("acz", len(eng(z)))], T.pw[:].indirect(T.cz[:, 0:7]), T.zi[:])
+
+    ncd = sum(2 * len(share(s, r)) for s in two(r)) + (2 * len(eng(z)) if z is not None else 0)
+    got = [down, ("apc", 2 * len(inner(pt))), ("acd", ncd)]
+
+    X = slice(W0 - 16, W0 + P)
+    m = scan([pp], T.pm[:], T.pw[:, X], T.pw[:, X], 0.0, Op.max, Op.max)
+    d0 = diag([m], T.pd[:, 0:128], T.pm[:, 16:144], 128)
+    d1 = diag([m], T.pd[:, 128:P], T.pm[:, 144:16 + P], P - 128)
+    l0 = tc([d0], T.il[:, 0:8], T.pd[:, 15:128:16])
+    l1 = tc([d1], T.il[:, 8:24], T.pd[:, 143:P:16])
+
+    def fin(b):
+        i = slice(128 * b, 128 * b + 128)
+        o = T.il[:, 8 * b:8 * b + 8]
+        dep = [l1 if b else l0] + got
+        return [pick(dep, T.fin[:, i], T.win[:], o), act(dep, T.fins[:, i], T.wins[:].indirect(o))]
+
+    def mul(b, h, deps):
+        k = NO * b + h
+        wi = slice(128 * k, 128 * k + 128)
+        i = slice(128 * b, 128 * b + 128)
+        return do("t", deps + qw, lambda: g.tensor.matmul_mx(
+            T.ps[:, 512 * k:512 * k + 128], T.wq[:, wi], T.ws[:, wi], T.fin[:, i], T.fins[:, i], True, True))
+
+    def out(b, h, mm):
+        k = NO * b + h
+        yi = slice(P * h + 128 * b, P * h + 128 * b + 128)
+        cp = tc([mm], T.ysb[:, yi], T.ps[:, 512 * k:512 * k + 128]) if h == 0 else act([mm], T.ysb[:, yi], T.ps[:, 512 * k:512 * k + 128])
+        dma("s", "dy", T.y[:, yi], T.ysb[:, yi], [cp])
+
+    y = []
+    for b in range(NB):
+        c = fin(b)
+        y.append([mul(b, h, c) for h in range(NO)])
+    for b in range(NB):
+        for h in range(NO):
+            out(b, h, y[b][h])
+
+    need("s", [("dy", total["dy"])])
+    g.wait_ge(T.sem.sent, sent[0])
+    need("g", [(s, total[s]) for s in total if s != "dy"])

@@ -2,10 +2,12 @@ from concourse.bass import DstId, RemoteDMATransfer
 from concourse.mybir import dt, AluOpType as Op, AxisListType, ActivationFunctionType as Act
 
 C, P, NB, NO, H = 192, 384, 3, 2, 112
-W0 = 1536
-TR = 3584
-FAR = 4096
-BIG = 1.0e6
+K = C // 64
+TR = 3200
+TW = 320
+FAR = 208
+PL = P + 8
+BIG = float(2 ** 20)
 WIN = 3 * H + 2 * C
 F32, I32, U16, U8, F8, BF = "float32", "int32", "uint16", "uint8", "float8_e4m3fn_x4", "bfloat16"
 
@@ -19,22 +21,20 @@ SCRATCH = {
     "raw": sb(C, F8), "raws": sb(C, U8), "comp": sb(C, F8), "comps": sb(C, U8),
     "sel2": sb(H, F8), "sel2s": sb(H, U8), "selz": sb(H, F8), "selzs": sb(H, U8),
     "win": sb(WIN, F8), "wins": sb(WIN, U8), "fin": sb(P, F8), "fins": sb(P, U8),
-    "pi": sb(1, I32), "pa": sb(1, I32), "pf": sb(1, F32), "c16": sb(16, F32), "tj": sb(16, F32), "tji": sb(26, I32),
-    "tjj": sb(26, I32), "m2": sb(16, F32), "ir": sb(C, F32), "op": sb(2 * C, F32), "vz": sb(2 * H, F32), "zi": sb(H, F32),
-    "mi": sb(16, I32), "mj": sb(16, I32), "mask": sb(P, F32), "rm": sb(64, BF), "rs": sb(26, F32),
-    "tb": sb(12, I32), "row1": sb(C, BF), "row": sb(C, BF), "T1": sb(64, BF), "A1": sb(96, BF), "B1": sb(64, BF),
-    "Z1": sb(64, BF), "ee": sb(27, F32), "uu": sb(26, F32), "z0": sb(26, F32), "zz": sb(26, F32),
-    "sx": sb(26, F32), "su": sb(26, U16), "kr": sb(11776, F32), "kd": sb(C, F32), "kl": sb(12, U16), "ke": sb(12, U16),
-    "er": sb(2 * C, F32), "sc": sb(C, F32),
-    "f2": sb(1, F32), "l2": sb(8, U16), "r2": sb(H, F32), "d0": sb(H, F32), "d2": sb(H, F32), "dz": sb(H, F32),
-    "t0": sb(8, U16), "t2": sb(8, U16), "tz": sb(8, U16), "rz": sb(H, F32),
-    "tl": sb(12, F32), "S": sb(1, F32), "pc": sb(1, F32), "jk": sb(C, F32), "js": sb(8, F32), "acc": sb(1, F32),
-    "lze": sb(8, U16), "pt": sb(12, U16), "po": sb(24, U16), "ct": sb(16, U16), "cz": sb(8, U16),
-    "pw": sb(14336, F32), "pm": sb(P + 16, F32), "pd": sb(P, F32), "il": sb(24, U16),
+    "pi": sb(1, I32), "pa": sb(3, I32), "pf": sb(3, F32), "pq": sb(1, F32), "c16": sb(16, F32), "t16": sb(64, F32),
+    "q3": sb(1, F32), "ro": sb(1, U16), "iw": sb(16 * K, F32), "tj": sb(16, F32), "tjz": sb(26, F32), "m2": sb(16, F32), "ir": sb(C, F32), "iq": sb(16 * K, F32), "ip": sb(16 * K, F32),
+    "bi": sb(12, F32), "bo": sb(12, U16), "mask": sb(PL, BF), "m64": sb(C, BF), "rm": sb(96, BF),
+    "vz": sb(16 * K, F32), "vy": sb(16 * K, F32), "vv": sb(4 * 16 * K, F32),
+    "tb": sb(12, I32), "T1": sb(64, BF), "A1": sb(64, BF), "B1": sb(64, BF), "Z1": sb(64, BF), "zf": sb(64, F32),
+    "uu": sb(26, F32), "z0": sb(26, F32), "rf": sb(16, F32), "rt": sb(4, U16), "sx": sb(26, F32), "su": sb(12, U16), "kr": sb(592, BF), "kd": sb(C, BF),
+    "kl": sb(12, U16), "ke": sb(12, U16), "bb": sb(C, F32), "er": sb(C + TW, F32), "sc": sb(C, F32), "dg": sb(C, F32),
+    "f2": sb(2, F32), "n2": sb(2, F32), "l2": sb(8, U16), "tx": sb(K, U16), "tl": sb(24, F32), "S": sb(1, F32),
+    "jk": sb(C - H, F32), "js": sb(8, F32), "lze": sb(8, U16), "acc": sb(1, F32),
+    "ct": sb(16, U16), "ot": sb(4 * K, U16), "oz": sb(K, U16), "a2": sb(2, F32), "az": sb(1, F32),
+    "pw": sb(TR + 8 * (TW + P), F32), "pd": sb(PL, F32), "mm": sb(24, F32), "mt": sb(24, F32), "my": sb(24, F32), "il": sb(24, U16),
     "ysb": sb(NO * P, F32), "ps": ("psum", [128, 512 * 6], F32),
 }
-SEMAPHORES = ["sv", "sa", "sg", "st", "dtab", "drow", "dx", "dw0", "dw1", "down", "dy", "sent",
-              "atot", "apt", "apc", "act", "acz", "acd"]
+SEMAPHORES = ["sv", "sa", "sg", "st", "dtab", "dx", "dw0", "dw1", "dy", "sent", "atot", "af2", "act", "acz", "apc", "acd"]
 
 
 def common(topo, src, dsts):
@@ -68,10 +68,19 @@ def rank_program(g, core, T, topo):
     def zed(q):
         return [d for d in (q - 1, q + 1) if 0 <= d < N and d != partner(q)]
 
+    def others(d):
+        return [s for s in range(max(0, d - 2), min(N, d + 3)) if s != d]
+
+    def part(q):
+        return [d for d in (partner(q),) if len(others(d)) == 4]
+
+    def full(q):
+        return zed(q) + [d for d in (partner(q),) if d not in part(q)]
+
     def seg(d):
         a, o = {}, 0
         for s in range(max(0, d - 2), min(N, d + 3)):
-            n = C if s in (d, partner(d)) else H
+            n = C if s == d or d in full(s) else H
             a[s] = (o, n)
             o += n
         return a
@@ -80,7 +89,7 @@ def rank_program(g, core, T, topo):
         return common(topo, cores[q], [c for c in cores if c != cores[q]])
 
     def inner(q):
-        return [e for e in topo.engines(cores[q], cores[partner(q)]) if e not in eng(q)] or eng(q)
+        return [e for e in topo.engines(cores[q], cores[partner(q)]) if e not in eng(q)][::2]
 
     def share(q, d):
         e, v = eng(q), two(q)
@@ -88,18 +97,20 @@ def rank_program(g, core, T, topo):
         return e[n * v.index(d):n * v.index(d) + n]
 
     def summed(d):
-        return list(range(d)) if d < half else list(range(d + 1, N))
+        return list(range(d + 2)) if d < half else list(range(N - 1, d - 3, -1))
 
     def slot(s, d):
-        if s in summed(d):
-            return half - len(summed(d)) + summed(d).index(s)
-        return 2 * half if s == partner(d) and s < d else None
+        k = 4 * summed(d).index(s)
+        return T.tl[:, k:k + 1]
+
+    def table(s, d, n=K):
+        k = 4 * others(d).index(s)
+        return T.ct[:, k:k + n]
 
     pt, me, E = partner(r), seg(r), eng(r)
     lo2 = r - 2 if r - 2 >= 0 else None
     hi2 = r + 2 if r + 2 < N else None
-    z = (zed(r) + [None])[0]
-    tr = float(TR * (1 + (r + r // half) % 2))
+    z = (part(r) + [None])[0]
     qs = {"v": g.vector, "a": g.scalar, "s": g.sync, "t": g.tensor, "g": g}
     home = {"v": "sv", "a": "sa", "t": "st", "g": "sg"}
     seen, total = {}, {}
@@ -148,11 +159,14 @@ def rank_program(g, core, T, topo):
     def scan(deps, out, a, b, init, op0, op1):
         return do("v", deps, lambda: V.tensor_tensor_scan(out, a, b, init, op0, op1))
 
-    def diag(deps, out, row, n):
-        return scan(deps, out, T.mask[:, 0:n], row, 0.0, Op.max, Op.min)
+    def diag(deps, out, mask, row):
+        return scan(deps, out, mask, row, 0.0, Op.max, Op.min)
 
-    def fill(ap, c):
-        return do("v", (), lambda: V.memset(ap, c))
+    def turn(deps, out, in_):
+        return do("v", deps, lambda: V.transpose(out, in_))
+
+    def fill(deps, ap, c):
+        return do("v", deps, lambda: V.memset(ap, c))
 
     def act(deps, out, in_, func=Act.Copy, **kw):
         return do("a", deps, lambda: A.activation(out, in_, func, **kw))
@@ -166,172 +180,194 @@ def rank_program(g, core, T, topo):
     def codes(ap):
         return ap.bitcast(dt.uint8)
 
-    shift = -P * z - 0.5 if z is not None else 0.0
+    def ee_(a, b):
+        return T.zf[:, 26 + a:26 + b]
 
-    def base(d):
-        return float(W0 - P * d) - shift
+    shift = -P * z - 0.5 if z is not None else 0.0
+    acc = T.acc[:]
 
     for k in range(8):
         dtab = dma("s" if k % 2 == 0 else "a", "dtab", T.tb[16 * k:16 * k + 16, :], T.cnt[:])
-    dx = dma("a", "dx", T.xt[:], T.x[:])
+    dx = dma("s", "dx", T.xt[:], T.x[:])
+    dw0 = dma("s", "dw0", T.wt[:, 0:1536], T.w[:, 0:1536])
+    dw1 = dma("s", "dw1", T.wt[:, 1536:3072], T.w[:, 1536:3072])
 
     flag = {"allow_small_or_imprecise_dtypes": True}
-    k4 = do("g", (), lambda: g.iota(T.mi[:], [[1, 16]], 0, 15))
-    k1 = do("g", (), lambda: g.iota(T.c16[:], [[16, 16]], 0, 0, **flag))
     k0 = do("g", (), lambda: g.iota(T.pi[:], [[0, 1]], 0, 1))
-    k5 = do("g", (), lambda: g.iota(T.tji[:], [[128, 26]], FAR * (1 + r % 2), 1))
-    k3 = do("g", (), lambda: g.iota(T.ir[:, 0:C], [[1, C]], 0, 0, **flag))
-    ft = fill(T.T1[:], 0.0)
-    u = fill(T.rm[:], 1.0)
-    v = ts([k4], T.mj[:], T.mi[:], 15, Op.bitwise_and)
-    fill(T.A1[:, 31:32], 0.0)
-    mk = ts([v], T.mask[:, 0:16], T.mj[:], 0.0, Op.is_equal, BIG, Op.mult)
-    fr = do("v", [u], lambda: V.memset(T.rm[:, 0:32:16], 0.0))
-    u = ts([k0], T.pa[:], T.pi[:], 15, Op.bitwise_and)
-    jj = ts([k5], T.tjj[:], T.tji[:], 16383 - 127 + 15, Op.bitwise_and)
-    pf = tc([u], T.pf[:], T.pa[:])
+    k4 = do("g", (), lambda: g.iota(T.t16[:], [[0, 4], [1, 16]], 0, 0, **flag))
+    k1 = do("g", (), lambda: g.iota(T.c16[:], [[16, 16]], 0, 0, **flag))
+    k5 = do("g", (), lambda: g.iota(T.bi[:], [[32, 6], [0, 2]], 0, 0, **flag))
+    k3 = do("g", (), lambda: g.iota(T.ir[:], [[1, C]], 0, 0, **flag))
+    k6 = do("g", (), lambda: g.iota(T.iq[:], [[128, K], [2, 16]], 0, 0, **flag))
+    ft = fill((), T.T1[:], 0.0)
+    u = fill((), T.rm[:], 1.0)
+    fz = fill((), T.zf[:], 0.0)
+    fr = fill([u], T.rm[:, 16:64:16], 0.0)
+    for k, m in enumerate((15, 16, 96)):
+        v = ts([k0], T.pa[:, k:k + 1], T.pi[:], m, Op.bitwise_and)
+    pf = tc([v], T.pf[:], T.pa[:])
+    row, odd, quarter = T.pf[:, 0:1], T.pf[:, 1:2], T.pf[:, 2:3]
+    mk = ts([pf, k4], T.mask[:, 0:64], T.t16[:], row, Op.is_equal, BIG, Op.mult)
+    bo = ts([pf, k5], T.bo[:], T.bi[:], odd, Op.add, 1.0 / 16, Op.mult)
+    ro = ts([pf], T.ro[:], quarter, K / 32, Op.mult, row, Op.add)
+    mk = tc([mk], T.mask[:, 64:128], T.mask[:, 0:64])
 
-    def const(deps, out, c):
-        return act([k1] + list(deps), out, T.c16[:, 0:1], Act.Identity, scale=0.0, bias=float(c))
+    j0 = act([pf, k1], T.tj[:], T.c16[:], Act.Identity, bias=row)
+    pq = act([pf], T.pq[:], quarter, Act.Identity, scale=0.5, bias=row)
+    act([j0], T.tjz[:, 0:14], T.tj[:, 0:14], Act.Identity, bias=float(TR + TW * r))
+    jz = act([j0], T.tjz[:, 14:26], T.tj[:, 0:12], Act.Identity, bias=float(FAR))
+    q3 = act([pf], T.q3[:], quarter, scale=float(K))
+    j3 = act([j0], T.m2[:], T.tj[:], Act.Identity, scale=-2.0, bias=-float(C - H))
+    act([k3], T.kr[:, 1:65], T.ir[:, 0:64], Act.Identity, bias=float(C))
+    kr = act([k3], T.kr[:, 65:C + 1], T.ir[:, 0:C - 64], Act.Identity, scale=2.0, bias=256.0)
+    act([k3], T.er[:, C:2 * C], T.ir[:], Act.Identity, bias=float(TR + TW * r))
+    ep = act([k3], T.er[:, 2 * C:C + TW], T.ir[:, 0:TW - C], Act.Identity, bias=float(TR + TW * r + C))
+    ip = act([k6], T.ip[:], T.iq[:], Act.Identity, bias=quarter)
+    iw = act([k3, q3], T.iw[:], T.ir[:, 0:16 * K], Act.Identity, scale=2.0, bias=T.q3[:])
+    order = [s for s in me if s != z]
 
-    fs = const((), T.tl[:, half:half + 1], shift if r < half else -(N * P + shift))
-    e0 = const((), T.er[:, 0:1], 0)
-    fz = const((), T.ee[:, 0:1], 0)
-    act([k1], T.rs[:, 0:13], T.c16[:, 0:13], Act.Identity, scale=0.0, bias=1.0)
-    act([k1], T.rs[:, 14:26], T.c16[:, 0:12], Act.Identity, scale=0.0, bias=1.0)
-    fz = const((), T.rs[:, 13:14], 0)
-    n = 16
-    while n < P:
-        w = min(n, P - n)
-        mk = act([mk], T.mask[:, n:n + w], T.mask[:, 0:w])
-        n += w
-        if n == 32:
-            j0 = act([pf], T.tj[:], T.c16[:], Act.Identity, bias=T.pf[:])
-        if n == 64:
-            kr = act([k3], T.kr[:, 0:C], T.ir[:, 0:C], Act.Identity, bias=float(C))
-            j3 = act([j0], T.m2[:], T.tj[:], Act.Identity, scale=-2.0, bias=-float(C - H))
-        if n == 256:
-            ep = act([k3], T.er[:, C:2 * C], T.ir[:, 0:C], Act.Identity, bias=tr)
+    def vals(s):
+        k = order.index(s)
+        return T.vv[:, 16 * K * k:16 * K * (k + 1)]
 
     a0 = tc([dtab, ft], T.T1[:, 0:12], T.tb[:])
     a1 = ts([dtab], T.T1[:, 14:26], T.tb[:], 0.0, Op.is_gt)
-    b1 = do("v", [a1, fr], lambda: V.transpose(T.A1[:, 32:96], T.T1[:]))
-    drow = dma("s", "drow", T.row1[0:1, :], T.A1[0:12, 32:48], [b1])
-    dw0 = dma("s", "dw0", T.wt[:, 0:1536], T.w[:, 0:1536])
-    dw1 = dma("s", "dw1", T.wt[:, 1536:3072], T.w[:, 1536:3072])
+    mk = tc([mk], T.mask[:, 128:256], T.mask[:, 0:128])
+    b1 = turn([a1], T.A1[:], T.T1[:])
     z0 = ts([a1], T.z0[:], T.T1[:, 0:26], 0.0, Op.is_equal)
-    b2 = scan([b1], T.B1[:], T.A1[:, 31:95], T.rm[:], 0.0, Op.add, Op.mult)
-    zz = tt([z0, jj], T.zz[:], T.z0[:], T.tjj[:], Op.mult)
-    b3 = do("v", [b2], lambda: V.transpose(T.Z1[:], T.B1[:]))
-    ee = scan([b3, fz], T.ee[:, 1:27], T.rs[:], T.Z1[:, 32:58], 0.0, Op.mult, Op.add)
-    uu = tt([b3, zz], T.uu[:], T.Z1[:, 0:26], T.zz[:], Op.add)
-    to = [d for d in range(N) if d != r and slot(r, d) is not None]
-    if to:
-        fused([ee], [(to, E, "atot", T.ee[:, 12:13], [T.tl[:, slot(r, d):slot(r, d) + 1] for d in to])])
-    sx = tt([uu, ee], T.sx[:], T.uu[:], T.ee[:, 0:26], Op.add)
-    f2 = act([ee], T.f2[:], T.ee[:, 26:27], Act.Relu, bias=-float(H))
-    if r >= half:
-        fs = act([ee], T.tl[:, half + 1:half + 2], T.ee[:, 12:13])
-    act([mk], T.pw[:, W0 - 16:W0 + P - 16], T.mask[:, 0:P], scale=0.0)
-    fp = act([mk], T.pw[:, W0 + P - 16:W0 + P], T.mask[:, 0:16], scale=0.0)
-    for k, s in enumerate((r, pt)):
-        op = act([k3], T.op[:, C * k:C * k + C], T.ir[:], Act.Identity, bias=float(me[s][0]))
-    for k, s in enumerate(two(r)):
-        vz = act([k3], T.vz[:, H * k:H * k + H], T.ir[:, 0:H], Act.Identity, bias=float(me[s][0]))
-    if z is not None:
-        zi = act([k3], T.zi[:], T.ir[:, 0:H], Act.Identity, bias=float(me[z][0]))
-    sxu = tc([sx], T.su[:], T.sx[:])
-    ks = tc([sxu, kr], T.kr[:].indirect(T.su[:, 14:26]), T.ir[:, 0:C])
+    b2 = scan([b1, fr], T.B1[:], T.rm[:, 32:96], T.A1[:], 0.0, Op.mult, Op.add)
+    zz = tt([z0, jz], T.z0[:], T.z0[:], T.tjz[:], Op.mult)
+    b3 = turn([b2], T.Z1[:], T.B1[:])
+    m64 = ts([k3, pq], T.m64[:, 0:64], T.ir[:, 0:64], T.pq[:], Op.is_equal, BIG, Op.mult)
+    ee = scan([b3, fz], ee_(1, 27), T.rm[:, 3:29], T.Z1[:, 32:58], 0.0, Op.mult, Op.add)
+    uu = tt([b3, zz], T.uu[:], T.Z1[:, 0:26], T.z0[:], Op.add)
+    to = [d for d in range(N) if d != r and r in summed(d)]
+    fused([ee], [(to, E, "atot", ee_(12, 13), [slot(r, d) for d in to])])
+    tc([m64], T.m64[:, 64:128], T.m64[:, 0:64])
+    sx = tt([uu, ee], T.sx[:], T.uu[:], ee_(0, 26), Op.add)
+    m64 = tc([m64], T.m64[:, 128:192], T.m64[:, 0:64])
     if hi2 is not None:
-        l2 = ts([f2, j0], T.l2[:, 0:7], T.tj[:, 0:7], T.f2[:], Op.add)
-    kd = diag([ks, mk], T.kd[:], T.kr[:, 0:C], C)
+        f2 = act([ee], T.f2[:], ee_(25, 27), Act.Relu, bias=-float(H))
+    rf = act([sx, ro], T.rf[:], T.sx[:].indirect(T.ro[:]))
+    bb = act([sx, bo], T.bb[:], T.sx[:].indirect(T.bo[:]))
+    fs = act([ee], slot(r, r), ee_(12, 13))
+    if hi2 is not None:
+        n2 = act([f2], T.n2[:], T.f2[:], Act.Identity, scale=-2.0, bias=2.0 * seg(hi2)[r][0])
+    ml = tc([mk], T.mask[:, 256:PL], T.mask[:, 0:PL - 256])
+    sxu = tc([sx], T.su[:], T.sx[:, 14:26])
+    fp = act([ml], T.pw[:, P * r:P * r + PL], T.mask[:], Act.Identity, scale=0.0, bias=BIG)
+    for s in order:
+        if s != lo2:
+            vv = act([ip, iw], vals(s), T.iw[:] if me[s][1] == C else T.ip[:], Act.Identity, bias=2.0 * me[s][0])
+    if z is not None:
+        vv = act([ip], T.vy[:], T.ip[:], Act.Identity, bias=2.0 * me[z][0] - (C - H))
     qx = do("v", [dx], lambda: V.quantize_mx(T.raw[:, 0:C], T.raws[:, 0:C], T.xt[:, 0:4 * C]))
-
-    ma, pa = me[r][0], seg(pt)[r][0]
-    pb = do("g", [drow], lambda: g.partition_broadcast(T.row[:], T.row1[0:1, :], 128))
-    fused([sxu], [([pt], E, "apt", T.su[:, 0:12], [T.pt[:]])])
-    dma("s", "down", codes(T.win[:, ma:ma + C]), codes(T.raw[:, 0:C]), [qx])
-    down = dma("s", "down", T.wins[:, ma:ma + C], T.raws[:, 0:C], [qx])
-
+    ks = tc([sxu, kr], T.kr[:].indirect(T.su[:]), T.ir[:])
+    er = turn([bb], T.er[:, 0:C], T.bb[:])
+    rt = tc([rf], T.rt[:], T.rf[:, 0:4])
+    kd = diag([ks, mk], T.kd[:], T.mask[:, 0:C], T.kr[:, 1:C + 1])
+    if hi2 is not None:
+        l2 = ts([f2, j0], T.l2[:, 0:7], T.tj[:, 0:7], T.f2[:, 1:2], Op.add)
     kl = ts([kd], T.kl[:], T.kd[:, 15:C:16], C - 1.0, Op.min)
     ke = tc([kd], T.ke[:], T.kd[:, 15:C:16])
-    er = scan([pb], T.er[:, 1:C], T.row[:, 0:C - 1], T.row[:, 0:C - 1], 0.0, Op.add, Op.max)
-    cq = pick([kl, qx], T.comp[:, 0:C], T.raw[:, 0:C], T.kl[:, 0:12])
-    cs = act([kl, qx], T.comps[:, 0:C], T.raws[:, 0:C].indirect(T.kl[:, 0:12]))
-    sc = act([er, e0, ep, ke], T.sc[:, 0:C], T.er[:, 0:2 * C].indirect(T.ke[:, 0:12]))
-    src, scl, tabs, tk = {}, {}, {}, {}
-    if hi2 is not None:
-        q2 = pick([l2, cq], T.sel2[:, 0:H], T.comp[:, 0:C], T.l2[:, 0:7])
-        src[hi2] = (T.sel2, q2)
-        r2 = act([sc, l2], T.r2[:], T.sc[:, 0:C].indirect(T.l2[:, 0:7]))
-    if lo2 is not None:
-        src[lo2] = (T.comp, cq)
-    at = {d: seg(d)[r][0] for d in seg(r)}
-    fused([src[d][1] for d in two(r)], [([d], share(r, d), "acd", codes(src[d][0][:, 0:H]), [codes(T.win[:, at[d]:at[d] + H])]) for d in two(r)])
-    fused([qx], [([pt], inner(r), "apc", codes(T.raw[:, 0:C]), [codes(T.win[:, pa:pa + C])])])
-    fused([qx], [([pt], inner(r), "apc", T.raws[:, 0:C], [T.wins[:, pa:pa + C]])])
 
-    na = sum(len(eng(s)) for s in range(N) if s != r and slot(s, r) is not None)
-    a, b = half - len(summed(r)), half + 1 if r < half else half + 2
-    tS = act([fs] + ([("atot", na)] if na else []), T.js[:, 0:b - a], T.tl[:, a:b], scale=1.0 if r < half else -1.0, accum_out=T.S[:])
+    cq = pick([kl, qx], T.comp[:], T.raw[:], T.kl[:])
+    sc = act([er, ep, ke], T.sc[:], T.er[:].indirect(T.ke[:]))
+    sm = summed(r)
+    tot = [fs, ("atot", sum(len(eng(s)) for s in sm if s != r))]
     if z is not None:
-        ac = act([tS, sc], T.jk[:, 0:C - H], T.sc[:, 1:C - H + 1], Act.Sign, bias=T.S[:], accum_out=T.acc[:])
-    if pt > r:
-        pc = act([tS, ee], T.pc[:], T.ee[:, 12:13], Act.Identity, bias=T.S[:])
-    else:
-        pc = act([tS], T.pc[:], T.tl[:, slot(pt, r):slot(pt, r) + 1], Act.Identity, scale=-1.0, bias=T.S[:])
-    if lo2 is not None:
-        tabs[lo2] = (T.t0, T.d0, diag([sc], T.d0[:], T.sc[:, 0:H], H))
+        n = r if r < half else N - r
+        tS = act(tot, T.js[:, 0:n], T.tl[:, 0:4 * n:4], Act.Identity, scale=1.0 if r < half else -1.0,
+                 bias=(shift if r < half else N * P + shift) / n, accum_out=T.S[:])
+        ac = act([tS, sc], T.jk[:], T.sc[:, 0:C - H], Act.Sign, bias=T.S[:], accum_out=acc)
+    cs = act([kl, qx], T.comps[:], T.raws[:].indirect(T.kl[:]))
+    dg = diag([sc, m64], T.dg[:], T.m64[:], T.sc[:])
+    scl = {}
     if hi2 is not None:
-        tabs[hi2] = (T.t2, T.d2, diag([r2], T.d2[:], T.r2[:], H))
-    qw = [quant(0, 384, dw0), quant(384, 768, dw1)]
-
-    if z is not None:
-        le = ts([ac, j3], T.lze[:, 0:7], T.m2[:, 0:7], T.acc[:], Op.add, -0.5, Op.mult)
-        rz = act([le], T.rz[:], T.sc[:, 0:C].indirect(T.lze[:, 0:7]))
+        q2 = pick([l2, cq], T.sel2[:], T.comp[:], T.l2[:, 0:7])
+        scl[hi2] = (T.sel2s, act([l2, cs], T.sel2s[:], T.comps[:].indirect(T.l2[:, 0:7])))
     if lo2 is not None:
         scl[lo2] = (T.comps, cs)
+    tx = tc([dg], T.tx[:], T.dg[:, 63:C:64])
+    qw = [quant(0, 384, dw0)]
+    n = len(sm)
+    ss = scan(tot, T.zf[:, 57:57 + n], T.rm[:, 64:64 + n], T.tl[:, 0:4 * n:4], 0.0 if r < half else float(N * P),
+              Op.mult, Op.add if r < half else Op.subtract)
+    if z is not None:
+        le = ts([ac, j3], T.lze[:, 0:7], T.m2[:, 0:7], acc, Op.add, -0.5, Op.mult)
+    tabs = ("act", sum(len(eng(s)) // (2 if r in full(s) and s + 2 < N else 1) for s in others(r)))
+
+    def places(s):
+        j = 56 + s if r < half else 57 + sm.index(s)
+        o = T.oz[:] if s == z else T.ot[:, K * order.index(s):K * order.index(s) + K]
+        return ts([ss] + ([] if s == r else [tabs]), o, T.rf[:, 0:K] if s == r else table(s, r), T.zf[:, j:j + 1], Op.add, -1.0, Op.add)
+
+    ot = places(r)
+    if z is not None:
+        qz = pick([le, cq], T.selz[:], T.comp[:], T.lze[:, 0:7])
+        qzs = act([le, cs], T.selzs[:], T.comps[:].indirect(T.lze[:, 0:7]))
+    if lo2 is not None:
+        vv = act([ip, ("af2", len(eng(lo2)) // 2)], vals(lo2), T.ip[:], Act.Identity, bias=T.a2[:, 1:2])
+    qw.append(quant(384, 768, dw1))
+    ma = me[r][0]
+    down = do("v", [dx], lambda: V.quantize_mx(T.win[:, ma:ma + C], T.wins[:, ma:ma + C], T.xt[:]))
+
+    at = {d: seg(d)[r][0] for d in seg(r)}
+    fl = full(r)
+
+    def way(d):
+        return inner(r) if d == pt else share(r, d) if d in two(r) else E
+
+    def sem(d):
+        return "apc" if d == pt else "acd"
+
+    src = {}
+    if lo2 is not None:
+        src[lo2] = (T.comp, cq)
     if hi2 is not None:
-        scl[hi2] = (T.sel2s, act([l2, cs], T.sel2s[:, 0:H], T.comps[:, 0:C].indirect(T.l2[:, 0:7])))
+        src[hi2] = (T.sel2, q2)
     if z is not None:
-        qzs = act([le, cs], T.selzs[:, 0:H], T.comps[:, 0:C].indirect(T.lze[:, 0:7]))
-    for d in tabs:
-        t, dd, tok = tabs[d]
-        tk[d] = ts([tok, tS], t[:, 0:7], dd[:, 15:H:16], T.S[:], Op.add, base(d), Op.add)
-    fused([tk[d] for d in two(r)], [([d], share(r, d), "act", tabs[d][0][:, 0:7], [T.ct[:, 7 * two(d).index(r):7 * two(d).index(r) + 7]]) for d in two(r)])
+        src[z] = (T.selz, qz)
+        scl[z] = (T.selzs, qzs)
+    fused([qx], [([d], way(d), sem(d), codes(T.raw[:]), [codes(T.win[:, at[d]:at[d] + C])]) for d in fl])
+    if hi2 is not None:
+        fused([rt, n2], [(fl, E[:len(E) // 2], "act", T.rt[:], [table(r, d, 4) for d in fl]), ([hi2], E[len(E) // 2:], "af2", T.n2[:], [T.a2[:]])])
+    else:
+        fused([rt], [(fl, E, "act", T.rt[:], [table(r, d, 4) for d in fl])])
+    fused([tx], [(two(r) + part(r), E, "act", T.tx[:], [table(r, d) for d in two(r) + part(r)])])
     if z is not None:
-        qz = pick([le, cq], T.selz[:, 0:H], T.comp[:, 0:C], T.lze[:, 0:7])
-        u = diag([rz], T.dz[:], T.rz[:], H)
-    oo = ts([tS, sx], T.po[:, 0:12], T.sx[:, 0:12], T.S[:], Op.add, base(r), Op.add)
-    if z is not None:
-        tz = ts([u], T.tz[:, 0:7], T.dz[:, 15:H:16], T.S[:], Op.add, base(z), Op.add)
-        fused([tz], [([z], E, "acz", T.tz[:, 0:7], [T.cz[:, 0:7]])])
-        fused([qz], [([z], E, "acd", codes(T.selz[:, 0:H]), [codes(T.win[:, at[z]:at[z] + H])])])
-    fused([scl[d][1] for d in two(r)], [([d], share(r, d), "acd", scl[d][0][:, 0:H], [T.wins[:, at[d]:at[d] + H]]) for d in two(r)])
-    if z is not None:
-        fused([qzs], [([z], E, "acd", T.selzs[:, 0:H], [T.wins[:, at[z]:at[z] + H]])])
+        fused([ac], [([z], way(z), "acz", acc, [T.az[:]])])
+    fused([src[d][1] for d in src], [([d], way(d), sem(d), codes(src[d][0][:, 0:H]), [codes(T.win[:, at[d]:at[d] + H])]) for d in src])
+    fused([qx], [([d], way(d), sem(d), T.raws[:], [T.wins[:, at[d]:at[d] + C]]) for d in fl])
+    fused([scl[d][1] for d in scl], [([d], way(d), sem(d), scl[d][0][:, 0:H], [T.wins[:, at[d]:at[d] + H]]) for d in scl])
 
-    po = ts([pc, ("apt", len(eng(pt)))], T.po[:, 12:24], T.pt[:], T.pc[:], Op.add, base(r), Op.add)
-    pp = tc([oo, po, fp, op], T.pw[:].indirect(T.po[:, 0:24]), T.op[:])
-    nt = len(two(r))
-    pp = tc([pp, vz, ("act", sum(len(share(s, r)) for s in two(r)))], T.pw[:].indirect(T.ct[:, 0:7 * nt]), T.vz[:, 0:H * nt])
+    for s in order:
+        if s != r:
+            ot = places(s)
     if z is not None:
-        pp = tc([pp, zi, ("acz", len(eng(z)))], T.pw[:].indirect(T.cz[:, 0:7]), T.zi[:])
+        oz = places(z)
+    no = len(order)
+    pp = tc([ot, vv, fp], T.pw[:].indirect(T.ot[:, 0:K * no]), T.vv[:, 0:16 * K * no])
+    if z is not None:
+        vz = act([("acz", len(inner(z)))], T.vz[:], T.vy[:], Act.Identity, bias=T.az[:])
+        pp = tc([pp, oz, vz], T.pw[:].indirect(T.oz[:]), T.vz[:])
 
-    ncd = sum(2 * len(share(s, r)) for s in two(r)) + (2 * len(eng(z)) if z is not None else 0)
+    ncd = sum(2 * len(share(s, r)) for s in two(r)) + sum(2 * len(eng(s)) for s in zed(r))
     got = [down, ("apc", 2 * len(inner(pt))), ("acd", ncd)]
 
-    X = slice(W0 - 16, W0 + P)
-    m = scan([pp], T.pm[:], T.pw[:, X], T.pw[:, X], 0.0, Op.max, Op.max)
-    d0 = diag([m], T.pd[:, 0:128], T.pm[:, 16:144], 128)
-    d1 = diag([m], T.pd[:, 128:P], T.pm[:, 144:16 + P], P - 128)
-    l0 = tc([d0], T.il[:, 0:8], T.pd[:, 15:128:16])
-    l1 = tc([d1], T.il[:, 8:24], T.pd[:, 143:P:16])
+    n = P + 5
+    m = diag([pp, ml], T.pd[:, 0:n], T.mask[:, 0:n], T.pw[:, P * r:P * r + n])
+    m = tt([m], T.mm[:], T.pd[:, 15:P:16], T.pd[:, 20:n:16], Op.min)
+    m = tt([m], T.mt[0:64, :], T.mm[0:64, :], T.mm[64:128, :], Op.min)
+    for k in (0, 32):
+        u = tt([m], T.my[k:k + 32, :], T.mt[0:32, :], T.mt[32:64, :], Op.min)
+    for k in (0, 64):
+        il = ts([u], T.il[k:k + 64, :], T.my[0:64, :], 0.5, Op.mult)
 
     def fin(b):
         i = slice(128 * b, 128 * b + 128)
         o = T.il[:, 8 * b:8 * b + 8]
-        dep = [l1 if b else l0] + got
+        dep = [il] + got
         return [pick(dep, T.fin[:, i], T.win[:], o), act(dep, T.fins[:, i], T.wins[:].indirect(o))]
 
     def mul(b, h, deps):
@@ -344,16 +380,17 @@ def rank_program(g, core, T, topo):
     def out(b, h, mm):
         k = NO * b + h
         yi = slice(P * h + 128 * b, P * h + 128 * b + 128)
-        cp = tc([mm], T.ysb[:, yi], T.ps[:, 512 * k:512 * k + 128]) if h == 0 else act([mm], T.ysb[:, yi], T.ps[:, 512 * k:512 * k + 128])
-        dma("s", "dy", T.y[:, yi], T.ysb[:, yi], [cp])
+        return (tc if h == 0 else act)([mm], T.ysb[:, yi], T.ps[:, 512 * k:512 * k + 128])
 
     y = []
     for b in range(NB):
         c = fin(b)
         y.append([mul(b, h, c) for h in range(NO)])
-    for b in range(NB):
+    for bs in ((0,), (1, 2)):
+        cp = [[out(b, h, y[b][h]) for h in range(NO)] for b in bs]
         for h in range(NO):
-            out(b, h, y[b][h])
+            yi = slice(P * h + 128 * bs[0], P * h + 128 * bs[-1] + 128)
+            dma("s", "dy", T.y[:, yi], T.ysb[:, yi], [cp[-1][h]])
 
     need("s", [("dy", total["dy"])])
     g.wait_ge(T.sem.sent, sent[0])

@@ -23,18 +23,18 @@ SCRATCH = {
     "win": sb(WIN, F8), "wins": sb(WIN, U8), "fin": sb(P, F8), "fins": sb(P, U8),
     "pi": sb(1, I32), "pa": sb(3, I32), "pf": sb(3, F32), "pq": sb(1, F32), "c16": sb(16, F32), "t16": sb(64, F32),
     "q3": sb(1, F32), "ro": sb(1, U16), "iw": sb(16 * K, F32), "tj": sb(16, F32), "tjz": sb(26, F32), "m2": sb(16, F32), "ir": sb(C, F32), "iq": sb(16 * K, F32), "ip": sb(16 * K, F32),
-    "bi": sb(12, F32), "bo": sb(12, U16), "mask": sb(PL, BF), "m64": sb(C, BF), "rm": sb(96, BF),
-    "vz": sb(16 * K, F32), "vy": sb(16 * K, F32), "vv": sb(4 * 16 * K, F32),
+    "bi": sb(12, F32), "bo": sb(12, U16), "mask": sb(PL, BF), "m64": sb(64, BF), "rm": sb(96, BF),
+    "vy": sb(16 * K, F32), "vv": sb(5 * 16 * K, F32),
     "tb": sb(12, I32), "T1": sb(64, BF), "A1": sb(64, BF), "B1": sb(64, BF), "Z1": sb(64, BF), "zf": sb(64, F32),
-    "uu": sb(26, F32), "z0": sb(26, F32), "rf": sb(16, F32), "rt": sb(4, U16), "sx": sb(26, F32), "su": sb(12, U16), "kr": sb(592, BF), "kd": sb(C, BF),
-    "kl": sb(12, U16), "ke": sb(12, U16), "bb": sb(C, F32), "er": sb(C + TW, F32), "sc": sb(C, F32), "dg": sb(C, F32),
-    "f2": sb(2, F32), "n2": sb(2, F32), "l2": sb(8, U16), "tx": sb(K, U16), "tl": sb(24, F32), "S": sb(1, F32),
+    "uu": sb(26, F32), "z0": sb(26, F32), "zz": sb(26, F32), "rf": sb(16, F32), "sx": sb(26, F32), "su": sb(12, U16), "kr": sb(592, BF), "kd": sb(C, BF),
+    "kl": sb(12, U16), "ke": sb(12, U16), "bb": sb(C, F32), "er": sb(C + TW, F32), "sc": sb(C, F32), "dg": sb(C + 2, F32), "sb": sb(3, F32), "tp": sb(1, F32),
+    "f2": sb(1, F32), "l2": sb(8, U16), "tl": sb(24, F32), "S": sb(1, F32),
     "jk": sb(C - H, F32), "js": sb(8, F32), "lze": sb(8, U16), "acc": sb(1, F32),
-    "ct": sb(16, U16), "ot": sb(4 * K, U16), "oz": sb(K, U16), "a2": sb(2, F32), "az": sb(1, F32),
-    "pw": sb(TR + 8 * (TW + P), F32), "pd": sb(PL, F32), "mm": sb(24, F32), "mt": sb(24, F32), "my": sb(24, F32), "il": sb(24, U16),
+    "ct": sb(32, F32), "ot": sb(5 * K, U16), "az": sb(1, F32),
+    "pw": sb(TR + 8 * (TW + P), F32), "pd": sb(PL, F32), "mt": sb(48, F32), "my": sb(24, F32), "il": sb(24, U16),
     "ysb": sb(NO * P, F32), "ps": ("psum", [128, 512 * 6], F32),
 }
-SEMAPHORES = ["sv", "sa", "sg", "st", "dtab", "dx", "dw0", "dw1", "dy", "sent", "atot", "af2", "act", "acz", "apc", "acd"]
+SEMAPHORES = ["sv", "sa", "sg", "st", "dtab", "dx", "dw0", "dw1", "dy", "sent", "atot", "atp", "act", "art", "acp", "acz", "apc", "acd"]
 
 
 def common(topo, src, dsts):
@@ -89,7 +89,7 @@ def rank_program(g, core, T, topo):
         return common(topo, cores[q], [c for c in cores if c != cores[q]])
 
     def inner(q):
-        return [e for e in topo.engines(cores[q], cores[partner(q)]) if e not in eng(q)][::2]
+        return [e for e in topo.engines(cores[q], cores[partner(q)]) if e not in eng(q)]
 
     def share(q, d):
         e, v = eng(q), two(q)
@@ -97,15 +97,15 @@ def rank_program(g, core, T, topo):
         return e[n * v.index(d):n * v.index(d) + n]
 
     def summed(d):
-        return list(range(d + 2)) if d < half else list(range(N - 1, d - 3, -1))
+        return list(range(d)) if d < half else list(range(d, N))
 
     def slot(s, d):
         k = 4 * summed(d).index(s)
         return T.tl[:, k:k + 1]
 
-    def table(s, d, n=K):
-        k = 4 * others(d).index(s)
-        return T.ct[:, k:k + n]
+    def table(s, d, a=0, b=K):
+        k = 8 * others(d).index(s)
+        return T.ct[:, k + a:k + b]
 
     pt, me, E = partner(r), seg(r), eng(r)
     lo2 = r - 2 if r - 2 >= 0 else None
@@ -177,6 +177,9 @@ def rank_program(g, core, T, topo):
     def quant(i, j, d):
         return do("v", [d], lambda: V.quantize_mx(T.wq[:, i:j], T.ws[:, i:j], T.wt[:, 4 * i:4 * j]))
 
+    def own(q, s):
+        return do("v", [dx], lambda: V.quantize_mx(q, s, T.xt[:]))
+
     def codes(ap):
         return ap.bitcast(dt.uint8)
 
@@ -186,7 +189,7 @@ def rank_program(g, core, T, topo):
     shift = -P * z - 0.5 if z is not None else 0.0
     acc = T.acc[:]
 
-    for k in range(8):
+    for k in range(4):
         dtab = dma("s" if k % 2 == 0 else "a", "dtab", T.tb[16 * k:16 * k + 16, :], T.cnt[:])
     dx = dma("s", "dx", T.xt[:], T.x[:])
     dw0 = dma("s", "dw0", T.wt[:, 0:1536], T.w[:, 0:1536])
@@ -224,93 +227,123 @@ def rank_program(g, core, T, topo):
     ep = act([k3], T.er[:, 2 * C:C + TW], T.ir[:, 0:TW - C], Act.Identity, bias=float(TR + TW * r + C))
     ip = act([k6], T.ip[:], T.iq[:], Act.Identity, bias=quarter)
     iw = act([k3, q3], T.iw[:], T.ir[:, 0:16 * K], Act.Identity, scale=2.0, bias=T.q3[:])
-    order = [s for s in me if s != z]
+    order = list(me)
 
     def vals(s):
         k = order.index(s)
         return T.vv[:, 16 * K * k:16 * K * (k + 1)]
 
-    a0 = tc([dtab, ft], T.T1[:, 0:12], T.tb[:])
-    a1 = ts([dtab], T.T1[:, 14:26], T.tb[:], 0.0, Op.is_gt)
+    lo, hi = slice(0, 64), slice(64, 128)
+    a0 = tc([dtab, ft], T.T1[lo, 0:12], T.tb[lo, :])
+    a1 = ts([dtab], T.T1[lo, 14:26], T.tb[lo, :], 0.0, Op.is_gt)
     mk = tc([mk], T.mask[:, 128:256], T.mask[:, 0:128])
-    b1 = turn([a1], T.A1[:], T.T1[:])
-    z0 = ts([a1], T.z0[:], T.T1[:, 0:26], 0.0, Op.is_equal)
-    b2 = scan([b1, fr], T.B1[:], T.rm[:, 32:96], T.A1[:], 0.0, Op.mult, Op.add)
-    zz = tt([z0, jz], T.z0[:], T.z0[:], T.tjz[:], Op.mult)
-    b3 = turn([b2], T.Z1[:], T.B1[:])
-    m64 = ts([k3, pq], T.m64[:, 0:64], T.ir[:, 0:64], T.pq[:], Op.is_equal, BIG, Op.mult)
+    b1 = turn([a1], T.A1[lo, :], T.T1[lo, :])
+    z0 = ts([a1], T.z0[lo, :], T.T1[lo, 0:26], 0.0, Op.is_equal)
+    b2 = scan([b1, fr], T.B1[lo, :], T.rm[lo, 32:96], T.A1[lo, :], 0.0, Op.mult, Op.add)
+    for h in (lo, hi):
+        zz = tt([z0, jz], T.zz[h, :], T.z0[lo, :], T.tjz[lo, :], Op.mult)
+    for h in (lo, hi):
+        b3 = turn([b2], T.Z1[h, :], T.B1[lo, :])
+    to = sorted((d for d in range(N) if d != r and r in summed(d)), key=lambda d: not part(d))
+    m64 = ts([k3, pq], T.m64[:], T.ir[:, 0:64], T.pq[:], Op.is_equal, BIG, Op.mult)
     ee = scan([b3, fz], ee_(1, 27), T.rm[:, 3:29], T.Z1[:, 32:58], 0.0, Op.mult, Op.add)
-    uu = tt([b3, zz], T.uu[:], T.Z1[:, 0:26], T.z0[:], Op.add)
-    to = [d for d in range(N) if d != r and r in summed(d)]
-    fused([ee], [(to, E, "atot", ee_(12, 13), [slot(r, d) for d in to])])
-    tc([m64], T.m64[:, 64:128], T.m64[:, 0:64])
+    uu = tt([b3, zz], T.uu[:], T.Z1[:, 0:26], T.zz[:], Op.add)
+    if z is not None:
+        qx = own(T.raw[:], T.raws[:])
     sx = tt([uu, ee], T.sx[:], T.uu[:], ee_(0, 26), Op.add)
-    m64 = tc([m64], T.m64[:, 128:192], T.m64[:, 0:64])
-    if hi2 is not None:
-        f2 = act([ee], T.f2[:], ee_(25, 27), Act.Relu, bias=-float(H))
+    f2 = act([ee], T.f2[:], ee_(26, 27), Act.Relu, bias=-float(H))
     rf = act([sx, ro], T.rf[:], T.sx[:].indirect(T.ro[:]))
     bb = act([sx, bo], T.bb[:], T.sx[:].indirect(T.bo[:]))
-    fs = act([ee], slot(r, r), ee_(12, 13))
-    if hi2 is not None:
-        n2 = act([f2], T.n2[:], T.f2[:], Act.Identity, scale=-2.0, bias=2.0 * seg(hi2)[r][0])
+    rf = act([rf], T.rf[:, K:K + 1], ee_(12, 13))
+    if r >= half:
+        act([ee], slot(r, r), ee_(12, 13))
+    act([ee], T.dg[:, C:C + 1], ee_(12, 13))
+    n2 = act([f2], T.dg[:, C + 1:C + 2], T.f2[:], scale=-2.0)
     ml = tc([mk], T.mask[:, 256:PL], T.mask[:, 0:PL - 256])
     sxu = tc([sx], T.su[:], T.sx[:, 14:26])
     fp = act([ml], T.pw[:, P * r:P * r + PL], T.mask[:], Act.Identity, scale=0.0, bias=BIG)
     for s in order:
-        if s != lo2:
+        if s not in (lo2, z):
             vv = act([ip, iw], vals(s), T.iw[:] if me[s][1] == C else T.ip[:], Act.Identity, bias=2.0 * me[s][0])
     if z is not None:
         vv = act([ip], T.vy[:], T.ip[:], Act.Identity, bias=2.0 * me[z][0] - (C - H))
-    qx = do("v", [dx], lambda: V.quantize_mx(T.raw[:, 0:C], T.raws[:, 0:C], T.xt[:, 0:4 * C]))
+    if z is None:
+        qx = own(T.raw[:], T.raws[:])
     ks = tc([sxu, kr], T.kr[:].indirect(T.su[:]), T.ir[:])
     er = turn([bb], T.er[:, 0:C], T.bb[:])
-    rt = tc([rf], T.rt[:], T.rf[:, 0:4])
     kd = diag([ks, mk], T.kd[:], T.mask[:, 0:C], T.kr[:, 1:C + 1])
     if hi2 is not None:
-        l2 = ts([f2, j0], T.l2[:, 0:7], T.tj[:, 0:7], T.f2[:, 1:2], Op.add)
-    kl = ts([kd], T.kl[:], T.kd[:, 15:C:16], C - 1.0, Op.min)
+        l2 = ts([f2, j0], T.l2[:, 0:7], T.tj[:, 0:7], T.f2[:], Op.add)
     ke = tc([kd], T.ke[:], T.kd[:, 15:C:16])
+    kl = ts([kd], T.kl[:], T.kd[:, 15:C:16], C - 1.0, Op.min)
 
     cq = pick([kl, qx], T.comp[:], T.raw[:], T.kl[:])
     sc = act([er, ep, ke], T.sc[:], T.er[:].indirect(T.ke[:]))
     sm = summed(r)
-    tot = [fs, ("atot", sum(len(eng(s)) for s in sm if s != r))]
+    n = len(sm)
+    at0, at1, atm = T.sb[:, 0:1], T.sb[:, 1:2], T.sb[:, 2:3]
+    if z is None:
+        cs = act([kl, qx], T.comps[:], T.raws[:].indirect(T.kl[:]))
+    tots = ("atot", len(E) * len([s for s in sm if s != r]))
+    if n:
+        tS = act([n2, tots], T.js[:, 0:n], T.tl[:, 0:4 * n:4], Act.Identity,
+                 scale=1.0 if r < half else -1.0, bias=(shift if r < half else N * P + shift) / n, accum_out=T.S[:])
     if z is not None:
-        n = r if r < half else N - r
-        tS = act(tot, T.js[:, 0:n], T.tl[:, 0:4 * n:4], Act.Identity, scale=1.0 if r < half else -1.0,
-                 bias=(shift if r < half else N * P + shift) / n, accum_out=T.S[:])
         ac = act([tS, sc], T.jk[:], T.sc[:, 0:C - H], Act.Sign, bias=T.S[:], accum_out=acc)
-    cs = act([kl, qx], T.comps[:], T.raws[:].indirect(T.kl[:]))
-    dg = diag([sc, m64], T.dg[:], T.m64[:], T.sc[:])
+    s0 = act([tS], at0, T.S[:], Act.Identity, bias=-shift - 1.0) if n else act([f2], at0, T.f2[:], Act.Identity, scale=0.0, bias=-1.0)
+    if z is not None:
+        cs = act([kl, qx], T.comps[:], T.raws[:].indirect(T.kl[:]))
+    s1 = act([s0], at1, ee_(12, 13), Act.Identity, bias=at0)
+
+    def here(s):
+        if r in full(s):
+            return ("art", sum(len(eng(q)) for q in others(r) if r in full(q)))
+        return ("acp", len(inner(s))) if s == z else ("act", sum(len(eng(q)) for q in two(r)))
+
+    def sum_of(s):
+        if s in sm:
+            return slot(s, r), tots
+        return (T.tp[:], ("atp", len(inner(s)))) if s == z else (table(s, r, K, K + 1), here(s))
+
+    def before():
+        return act([s0, sum_of(r - 1)[1]], atm, sum_of(r - 1)[0], Act.Identity, scale=-1.0, bias=at0)
+
+    early = r - 1 in sm + [z]
+    if lo2 is not None and early:
+        s2 = before()
+    for c in range(K):
+        tx = diag([sc, m64], T.dg[:, c:C:K], T.m64[:], T.sc[:, 64 * c:64 * c + 64])
     scl = {}
     if hi2 is not None:
         q2 = pick([l2, cq], T.sel2[:], T.comp[:], T.l2[:, 0:7])
         scl[hi2] = (T.sel2s, act([l2, cs], T.sel2s[:], T.comps[:].indirect(T.l2[:, 0:7])))
     if lo2 is not None:
         scl[lo2] = (T.comps, cs)
-    tx = tc([dg], T.tx[:], T.dg[:, 63:C:64])
     qw = [quant(0, 384, dw0)]
-    n = len(sm)
-    ss = scan(tot, T.zf[:, 57:57 + n], T.rm[:, 64:64 + n], T.tl[:, 0:4 * n:4], 0.0 if r < half else float(N * P),
-              Op.mult, Op.add if r < half else Op.subtract)
     if z is not None:
         le = ts([ac, j3], T.lze[:, 0:7], T.m2[:, 0:7], acc, Op.add, -0.5, Op.mult)
-    tabs = ("act", sum(len(eng(s)) // (2 if r in full(s) and s + 2 < N else 1) for s in others(r)))
-
-    def places(s):
-        j = 56 + s if r < half else 57 + sm.index(s)
-        o = T.oz[:] if s == z else T.ot[:, K * order.index(s):K * order.index(s) + K]
-        return ts([ss] + ([] if s == r else [tabs]), o, T.rf[:, 0:K] if s == r else table(s, r), T.zf[:, j:j + 1], Op.add, -1.0, Op.add)
-
-    ot = places(r)
+    ma = me[r][0]
+    down = own(T.win[:, ma:ma + C], T.wins[:, ma:ma + C])
     if z is not None:
         qz = pick([le, cq], T.selz[:], T.comp[:], T.lze[:, 0:7])
         qzs = act([le, cs], T.selzs[:], T.comps[:].indirect(T.lze[:, 0:7]))
     if lo2 is not None:
-        vv = act([ip, ("af2", len(eng(lo2)) // 2)], vals(lo2), T.ip[:], Act.Identity, bias=T.a2[:, 1:2])
+        if not early:
+            s2 = before()
+        vv = act([ip, here(lo2)], vals(lo2), T.ip[:], Act.Identity, bias=table(lo2, r, K + 1, K + 2))
+
+    def places(s):
+        o = T.ot[:, K * order.index(s):K * order.index(s) + K]
+        if s == r:
+            return ts([s0], o, T.rf[:, 0:K], at0, Op.add)
+        if s == r + 1:
+            return ts([s1, here(s)], o, table(s, r), at1, Op.add)
+        if s == r + 2:
+            return ts([s1, here(s), sum_of(r + 1)[1]], o, table(s, r), at1, Op.add, sum_of(r + 1)[0], Op.add)
+        return ts([s0 if s == r - 1 else s2, here(s)], o, table(s, r), at0 if s == r - 1 else atm, Op.add, table(s, r, K, K + 1), Op.subtract)
+
+    ot = places(r)
     qw.append(quant(384, 768, dw1))
-    ma = me[r][0]
-    down = do("v", [dx], lambda: V.quantize_mx(T.win[:, ma:ma + C], T.wins[:, ma:ma + C], T.xt[:]))
 
     at = {d: seg(d)[r][0] for d in seg(r)}
     fl = full(r)
@@ -329,38 +362,40 @@ def rank_program(g, core, T, topo):
     if z is not None:
         src[z] = (T.selz, qz)
         scl[z] = (T.selzs, qzs)
-    fused([qx], [([d], way(d), sem(d), codes(T.raw[:]), [codes(T.win[:, at[d]:at[d] + C])]) for d in fl])
-    if hi2 is not None:
-        fused([rt, n2], [(fl, E[:len(E) // 2], "act", T.rt[:], [table(r, d, 4) for d in fl]), ([hi2], E[len(E) // 2:], "af2", T.n2[:], [T.a2[:]])])
-    else:
-        fused([rt], [(fl, E, "act", T.rt[:], [table(r, d, 4) for d in fl])])
-    fused([tx], [(two(r) + part(r), E, "act", T.tx[:], [table(r, d) for d in two(r) + part(r)])])
-    if z is not None:
-        fused([ac], [([z], way(z), "acz", acc, [T.az[:]])])
-    fused([src[d][1] for d in src], [([d], way(d), sem(d), codes(src[d][0][:, 0:H]), [codes(T.win[:, at[d]:at[d] + H])]) for d in src])
-    fused([qx], [([d], way(d), sem(d), T.raws[:], [T.wins[:, at[d]:at[d] + C]]) for d in fl])
-    fused([scl[d][1] for d in scl], [([d], way(d), sem(d), scl[d][0][:, 0:H], [T.wins[:, at[d]:at[d] + H]]) for d in scl])
+    far = sorted(two(r), key=lambda d: not part(d))
+    calls = {
+        "total": ([ee], [(to, inner(r) if to == [pt] and z is not None else E, "atot", ee_(12, 13), [slot(r, d) for d in to])] if to else []),
+        "late total": ([ee], [([d], inner(r), "atp", ee_(12, 13), [T.tp[:]]) for d in part(r) if d not in to]),
+        "all codes": ([qx], [([d], way(d), sem(d), codes(T.raw[:]), [codes(T.win[:, at[d]:at[d] + C])]) for d in fl]),
+        "all scales": ([qx], [([d], way(d), sem(d), T.raws[:], [T.wins[:, at[d]:at[d] + C]]) for d in fl]),
+        "all table": ([rf], [(fl, E, "art", T.rf[:, 0:K + 1], [table(r, d, 0, K + 1) for d in fl])]),
+        "table": ([tx, n2], [(far, E, "act", T.dg[:, C - K:C + 2], [table(r, d, 0, K + 2) for d in far])]
+                  + [([d], inner(r), "acp", T.dg[:, C - K:C + 2], [table(r, d, 0, K + 2)]) for d in part(r)]),
+        "shift": ([ac], [([z], inner(r), "acz", acc, [T.az[:]])]) if z is not None else None,
+        "codes": ([src[d][1] for d in src], [([d], way(d), sem(d), codes(src[d][0][:, 0:H]), [codes(T.win[:, at[d]:at[d] + H])]) for d in src]),
+        "scales": ([scl[d][1] for d in scl], [([d], way(d), sem(d), scl[d][0][:, 0:H], [T.wins[:, at[d]:at[d] + H]]) for d in scl]),
+    }
+    for k in (("total", "all codes", "all table", "late total", "table", "shift", "all scales", "codes", "scales") if z is not None else
+              ("total", "all codes", "all table", "table", "codes", "all scales", "scales")):
+        if calls[k][1]:
+            fused(*calls[k])
 
-    for s in order:
+    if z is not None:
+        vv = act([("acz", len(inner(z)))], vals(z), T.vy[:], Act.Identity, bias=T.az[:])
+    for s in sorted(order, key=lambda s: s in two(r)):
         if s != r:
             ot = places(s)
-    if z is not None:
-        oz = places(z)
     no = len(order)
     pp = tc([ot, vv, fp], T.pw[:].indirect(T.ot[:, 0:K * no]), T.vv[:, 0:16 * K * no])
-    if z is not None:
-        vz = act([("acz", len(inner(z)))], T.vz[:], T.vy[:], Act.Identity, bias=T.az[:])
-        pp = tc([pp, oz, vz], T.pw[:].indirect(T.oz[:]), T.vz[:])
 
     ncd = sum(2 * len(share(s, r)) for s in two(r)) + sum(2 * len(eng(s)) for s in zed(r))
     got = [down, ("apc", 2 * len(inner(pt))), ("acd", ncd)]
 
-    n = P + 5
-    m = diag([pp, ml], T.pd[:, 0:n], T.mask[:, 0:n], T.pw[:, P * r:P * r + n])
-    m = tt([m], T.mm[:], T.pd[:, 15:P:16], T.pd[:, 20:n:16], Op.min)
-    m = tt([m], T.mt[0:64, :], T.mm[0:64, :], T.mm[64:128, :], Op.min)
+    m = diag([pp, ml], T.pd[:], T.mask[:], T.pw[:, P * r:P * r + PL])
+    back = slice(PL - 1, 14, -8)
+    m = scan([m], T.mt[lo, ::-1], T.pd[lo, back], T.pd[hi, back], BIG, Op.min, Op.min)
     for k in (0, 32):
-        u = tt([m], T.my[k:k + 32, :], T.mt[0:32, :], T.mt[32:64, :], Op.min)
+        u = tt([m], T.my[k:k + 32, :], T.mt[0:32, ::2], T.mt[32:64, ::2], Op.min)
     for k in (0, 64):
         il = ts([u], T.il[k:k + 64, :], T.my[0:64, :], 0.5, Op.mult)
 

@@ -4,11 +4,12 @@ from concourse.mybir import dt, AluOpType as Op, AxisListType, ActivationFunctio
 C, P, NB, NO, H = 192, 384, 3, 2, 112
 K = C // 64
 TR = 3200
-TW = 320
 FAR = 208
 PL = P + 8
 BIG = float(2 ** 20)
 WIN = 3 * H + 2 * C
+Q = 16 * K
+TOT = 63
 F32, I32, U16, U8, F8, BF = "float32", "int32", "uint16", "uint8", "float8_e4m3fn_x4", "bfloat16"
 
 
@@ -21,20 +22,21 @@ SCRATCH = {
     "raw": sb(C, F8), "raws": sb(C, U8), "comp": sb(C, F8), "comps": sb(C, U8),
     "sel2": sb(H, F8), "sel2s": sb(H, U8), "selz": sb(H, F8), "selzs": sb(H, U8),
     "win": sb(WIN, F8), "wins": sb(WIN, U8), "fin": sb(P, F8), "fins": sb(P, U8),
-    "pi": sb(1, I32), "pa": sb(3, I32), "pf": sb(3, F32), "pq": sb(1, F32), "c16": sb(16, F32), "t16": sb(64, F32),
-    "q3": sb(1, F32), "ro": sb(1, U16), "iw": sb(16 * K, F32), "tj": sb(16, F32), "tjz": sb(26, F32), "m2": sb(16, F32), "ir": sb(C, F32), "iq": sb(16 * K, F32), "ip": sb(16 * K, F32),
-    "bi": sb(12, F32), "bo": sb(12, U16), "mask": sb(PL, BF), "m64": sb(64, BF), "rm": sb(96, BF),
-    "vy": sb(16 * K, F32), "vv": sb(5 * 16 * K, F32),
-    "tb": sb(12, I32), "T1": sb(64, BF), "A1": sb(64, BF), "B1": sb(64, BF), "Z1": sb(64, BF), "zf": sb(64, F32),
-    "uu": sb(26, F32), "z0": sb(26, F32), "zz": sb(26, F32), "rf": sb(16, F32), "sx": sb(26, F32), "su": sb(12, U16), "kr": sb(592, BF), "kd": sb(C, BF),
-    "kl": sb(12, U16), "ke": sb(12, U16), "bb": sb(C, F32), "er": sb(C + TW, F32), "sc": sb(C, F32), "dg": sb(C + 2, F32), "sb": sb(3, F32), "tp": sb(1, F32),
-    "f2": sb(1, F32), "l2": sb(8, U16), "tl": sb(24, F32), "S": sb(1, F32),
-    "jk": sb(C - H, F32), "js": sb(8, F32), "lze": sb(8, U16), "acc": sb(1, F32),
-    "ct": sb(32, F32), "ot": sb(5 * K, U16), "az": sb(1, F32),
-    "pw": sb(TR + 8 * (TW + P), F32), "pd": sb(PL, F32), "mt": sb(48, F32), "my": sb(24, F32), "il": sb(24, U16),
+    "pi": sb(1, I32), "pa": sb(3, I32), "pf": sb(3, F32), "pr": sb(3, F32), "ro": sb(1, U16), "ko": sb(1, U16),
+    "c16": sb(28, F32), "tj": sb(28, F32), "ir": sb(C, F32), "bi": sb(12, F32), "bo": sb(12, U16), "mask": sb(PL, BF), "rm": sb(96, BF),
+    "iq": sb(Q, F32), "ip": sb(Q, F32), "m2": sb(7, F32), "vv": sb(5 * Q, F32),
+    "tb": sb(12, I32), "T1": sb(64, BF), "A1": sb(64, BF), "B1": sb(64, BF), "Z1": sb(64, BF), "R1": sb(64, BF), "R2": sb(32, BF),
+    "zf": sb(32, F32), "uu": sb(28, F32), "z0": sb(28, F32), "zz": sb(28, F32), "sx": sb(28, F32), "su": sb(12, U16),
+    "kr": sb(592, BF), "kd": sb(C + 1, BF), "kl": sb(12, U16), "ke": sb(16, U16), "bb": sb(C, F32), "er": sb(C + Q, F32),
+    "sc": sb(Q, F32), "dg": sb(TOT + 61, F32), "sb": sb(5, F32), "tp": sb(1, F32), "l2": sb(8, U16),
+    "jk": sb(C - H, F32), "sf": sb(C - H, F32), "sg": sb(C - H, F32), "cz": sb(1, F32), "js": sb(16, F32), "jt": sb(8, F32), "lze": sb(8, U16), "acc": sb(1, F32),
+    "ct": sb(32, F32), "ot": sb(16, U16), "az": sb(1, F32),
+    "pw": sb(TR + 8 * (C + P), F32), "pd": sb(PL, F32), "mt": sb(48, F32), "my": sb(24, F32), "il": sb(24, U16),
     "ysb": sb(NO * P, F32), "ps": ("psum", [128, 512 * 6], F32),
 }
-SEMAPHORES = ["sv", "sa", "sg", "st", "dtab", "dx", "dw0", "dw1", "dy", "sent", "atot", "atp", "act", "art", "acp", "acz", "apc", "acd"]
+SEMAPHORES = ["sv", "sa", "sg", "st", "dtab", "dx", "dw0", "dw1", "dy", "sent", "atot", "atp", "act", "art", "acp", "acz", "acd", "asd"]
+ORDER = ((("total", "all table", "all codes"), ("table", "all scales", "codes", "scales")),
+         (("total", "late total", "all codes", "all table", "all scales"), ("table", "shift", "codes", "scales", "part codes", "part scales")))
 
 
 def common(topo, src, dsts):
@@ -85,6 +87,9 @@ def rank_program(g, core, T, topo):
             o += n
         return a
 
+    def ranked(d):
+        return sorted(seg(d), key=lambda s: (seg(d)[s][1] == H, s != d, s == d + 2, s not in part(d)))
+
     def eng(q):
         return common(topo, cores[q], [c for c in cores if c != cores[q]])
 
@@ -100,17 +105,22 @@ def rank_program(g, core, T, topo):
         return list(range(d)) if d < half else list(range(d, N))
 
     def slot(s, d):
-        k = 4 * summed(d).index(s)
-        return T.tl[:, k:k + 1]
+        k = TOT + 20 * (summed(d).index(s) + (d < half))
+        return T.dg[:, k:k + 1]
 
     def table(s, d, a=0, b=K):
-        k = 8 * others(d).index(s)
+        k = 8 * others(d).index(s) + 1
         return T.ct[:, k + a:k + b]
+
+    def table_sum(s, d):
+        return table(s, d, -1, 0) if d in full(s) else table(s, d, K, K + 1)
 
     pt, me, E = partner(r), seg(r), eng(r)
     lo2 = r - 2 if r - 2 >= 0 else None
     hi2 = r + 2 if r + 2 < N else None
     z = (part(r) + [None])[0]
+    order = ranked(r)
+    early = 2
     qs = {"v": g.vector, "a": g.scalar, "s": g.sync, "t": g.tensor, "g": g}
     home = {"v": "sv", "a": "sa", "t": "st", "g": "sg"}
     seen, total = {}, {}
@@ -140,10 +150,14 @@ def rank_program(g, core, T, topo):
     sent = [0]
 
     def fused(deps, trs):
-        need("g", deps)
-        g.remote_dma_fused([RemoteDMATransfer(dst_ids=[dst(cores[d]) for d in ds], dma_engine_mask=bits(e), remote_sem=T.sem[sem],
-                                              srcs=[a], dsts=b) for ds, e, sem, a, b in trs], local_sem=T.sem.sent)
-        sent[0] += sum(len(e) for ds, e, sem, a, b in trs)
+        if trs:
+            need("g", deps)
+            g.remote_dma_fused([RemoteDMATransfer(dst_ids=[dst(cores[d]) for d in ds], dma_engine_mask=bits(e), remote_sem=T.sem[sem],
+                                                  srcs=[a], dsts=b) for ds, e, sem, a, b in trs], local_sem=T.sem.sent)
+            sent[0] += sum(len(e) for ds, e, sem, a, b in trs)
+
+    def iota(out, pattern, base):
+        return do("g", (), lambda: g.iota(out, pattern, base, 0, allow_small_or_imprecise_dtypes=True))
 
     def tc(deps, out, in_):
         return do("v", deps, lambda: V.tensor_copy(out, in_))
@@ -168,132 +182,157 @@ def rank_program(g, core, T, topo):
     def fill(deps, ap, c):
         return do("v", deps, lambda: V.memset(ap, c))
 
-    def act(deps, out, in_, func=Act.Copy, **kw):
+    def act(deps, out, in_, func=Act.Identity, **kw):
         return do("a", deps, lambda: A.activation(out, in_, func, **kw))
 
     def pick(deps, out, in_, o):
         return tc(deps, out.bitcast(dt.uint32), in_.bitcast(dt.uint32).indirect(o))
 
-    def quant(i, j, d):
-        return do("v", [d], lambda: V.quantize_mx(T.wq[:, i:j], T.ws[:, i:j], T.wt[:, 4 * i:4 * j]))
+    def picks(deps, out, in_, o):
+        return act(deps, out, in_.indirect(o), Act.Copy)
 
-    def own(q, s):
-        return do("v", [dx], lambda: V.quantize_mx(q, s, T.xt[:]))
+    qw = []
+
+    def quant(k, n=1):
+        i, j = 128 * k, 128 * (k + n)
+        qw.extend([do("v", dw[k // NO:(k + n - 1) // NO + 1], lambda: V.quantize_mx(T.wq[:, i:j], T.ws[:, i:j], T.wt[:, 4 * i:4 * j]))] * n)
+
+    def own(q, s, k, a=0, b=C, deps=()):
+        return do("v", [dx, *deps], lambda: V.quantize_mx(q[:, k + a:k + b], s[:, k + a:k + b], T.xt[:, 4 * a:4 * b]))
 
     def codes(ap):
         return ap.bitcast(dt.uint8)
 
-    def ee_(a, b):
-        return T.zf[:, 26 + a:26 + b]
+    def vals(s):
+        k = order.index(s)
+        return T.vv[:, Q * k:Q * (k + 1)]
 
-    shift = -P * z - 0.5 if z is not None else 0.0
-    acc = T.acc[:]
+    acc, tot, nw = T.acc[:], T.dg[:, TOT:TOT + 1], T.sx[:, 12:13]
+    to = sorted((d for d in range(N) if d != r and r in summed(d)), key=lambda d: not part(d))
+    lo, hi = slice(0, 64), slice(64, 128)
+    at = {d: seg(d)[r][0] for d in seg(r)}
+    fl = full(r)
+
+    def way(d):
+        return inner(r) if d == pt else share(r, d) if d in two(r) else E
 
     for k in range(4):
         dtab = dma("s" if k % 2 == 0 else "a", "dtab", T.tb[16 * k:16 * k + 16, :], T.cnt[:])
     dx = dma("s", "dx", T.xt[:], T.x[:])
-    dw0 = dma("s", "dw0", T.wt[:, 0:1536], T.w[:, 0:1536])
-    dw1 = dma("s", "dw1", T.wt[:, 1536:3072], T.w[:, 1536:3072])
+    dw = [dma("s", "dw0", T.wt[:, 0:1024], T.w[:, 0:1024])] + [dma("s", "dw1", T.wt[:, 1024:3072], T.w[:, 1024:3072])] * 2
 
-    flag = {"allow_small_or_imprecise_dtypes": True}
     k0 = do("g", (), lambda: g.iota(T.pi[:], [[0, 1]], 0, 1))
-    k4 = do("g", (), lambda: g.iota(T.t16[:], [[0, 4], [1, 16]], 0, 0, **flag))
-    k1 = do("g", (), lambda: g.iota(T.c16[:], [[16, 16]], 0, 0, **flag))
-    k5 = do("g", (), lambda: g.iota(T.bi[:], [[32, 6], [0, 2]], 0, 0, **flag))
-    k3 = do("g", (), lambda: g.iota(T.ir[:], [[1, C]], 0, 0, **flag))
-    k6 = do("g", (), lambda: g.iota(T.iq[:], [[128, K], [2, 16]], 0, 0, **flag))
+    k1 = iota(T.c16[:], [[TR + C * r - FAR - 32, 2], [16, 14]], FAR)
+    k4 = iota(T.kr[:, 1:C + 1], [[16, K], [0, 4], [1, 16]], C)
+    k5 = iota(T.bi[:], [[32, 6], [0, 2]], 0)
+    k3 = iota(T.ir[:], [[1, C]], 0)
+    k6 = iota(T.iq[:], [[128, K], [2, 16]], 0)
     ft = fill((), T.T1[:], 0.0)
     u = fill((), T.rm[:], 1.0)
-    fz = fill((), T.zf[:], 0.0)
-    fr = fill([u], T.rm[:, 16:64:16], 0.0)
+    fz = fill((), T.zf[:, 0:1], 0.0)
+    fj = fill((), T.tj[:, 12:13], 0.0)
     for k, m in enumerate((15, 16, 96)):
         v = ts([k0], T.pa[:, k:k + 1], T.pi[:], m, Op.bitwise_and)
+    fr = fill([u], T.rm[:, 16:64:16], 0.0)
     pf = tc([v], T.pf[:], T.pa[:])
     row, odd, quarter = T.pf[:, 0:1], T.pf[:, 1:2], T.pf[:, 2:3]
-    mk = ts([pf, k4], T.mask[:, 0:64], T.t16[:], row, Op.is_equal, BIG, Op.mult)
-    bo = ts([pf, k5], T.bo[:], T.bi[:], odd, Op.add, 1.0 / 16, Op.mult)
-    ro = ts([pf], T.ro[:], quarter, K / 32, Op.mult, row, Op.add)
-    mk = tc([mk], T.mask[:, 64:128], T.mask[:, 0:64])
+    fp = fill((), T.pw[:, P * r:P * r + PL], BIG)
+    ts([pf], T.pr[:, 0:1], row, K - 1.0, Op.min, 4.0, Op.mult)
+    pr = ts([pf], T.pr[:, 1:2], row, K - 1.0, Op.min, 64.0, Op.mult)
 
-    j0 = act([pf, k1], T.tj[:], T.c16[:], Act.Identity, bias=row)
-    pq = act([pf], T.pq[:], quarter, Act.Identity, scale=0.5, bias=row)
-    act([j0], T.tjz[:, 0:14], T.tj[:, 0:14], Act.Identity, bias=float(TR + TW * r))
-    jz = act([j0], T.tjz[:, 14:26], T.tj[:, 0:12], Act.Identity, bias=float(FAR))
-    q3 = act([pf], T.q3[:], quarter, scale=float(K))
-    j3 = act([j0], T.m2[:], T.tj[:], Act.Identity, scale=-2.0, bias=-float(C - H))
-    act([k3], T.kr[:, 1:65], T.ir[:, 0:64], Act.Identity, bias=float(C))
-    kr = act([k3], T.kr[:, 65:C + 1], T.ir[:, 0:C - 64], Act.Identity, scale=2.0, bias=256.0)
-    act([k3], T.er[:, C:2 * C], T.ir[:], Act.Identity, bias=float(TR + TW * r))
-    ep = act([k3], T.er[:, 2 * C:C + TW], T.ir[:, 0:TW - C], Act.Identity, bias=float(TR + TW * r + C))
-    ip = act([k6], T.ip[:], T.iq[:], Act.Identity, bias=quarter)
-    iw = act([k3, q3], T.iw[:], T.ir[:, 0:16 * K], Act.Identity, scale=2.0, bias=T.q3[:])
-    order = list(me)
+    act([pf, k1], T.tj[:, 0:12], T.c16[:, 0:12], bias=row)
+    j0 = act([pf, k1], T.tj[:, 13:28], T.c16[:, 13:28], bias=row)
+    p2 = act([pf], T.pr[:, 2:3], row, bias=float(C))
+    if z is not None:
+        j3 = act([j0], T.m2[:], T.tj[:, 0:7], scale=-2.0, bias=2.0 * FAR - (C - H))
 
-    def vals(s):
-        k = order.index(s)
-        return T.vv[:, 16 * K * k:16 * K * (k + 1)]
-
-    lo, hi = slice(0, 64), slice(64, 128)
-    a0 = tc([dtab, ft], T.T1[lo, 0:12], T.tb[lo, :])
-    a1 = ts([dtab], T.T1[lo, 14:26], T.tb[lo, :], 0.0, Op.is_gt)
-    mk = tc([mk], T.mask[:, 128:256], T.mask[:, 0:128])
+    a0 = tc([dtab, ft], T.T1[lo, 20:32], T.tb[lo, :])
+    a1 = ts([dtab], T.T1[lo, 4:16], T.tb[lo, :], 0.0, Op.is_gt)
+    ko = ts([pr], T.ko[:], quarter, 0.5, Op.mult, T.pr[:, 1:2], Op.add)
+    t1 = scan([a0, fr], T.R1[lo, 20:64], T.rm[lo, 52:96], T.T1[lo, 20:64], 0.0, Op.mult, Op.add)
     b1 = turn([a1], T.A1[lo, :], T.T1[lo, :])
-    z0 = ts([a1], T.z0[lo, :], T.T1[lo, 0:26], 0.0, Op.is_equal)
-    b2 = scan([b1, fr], T.B1[lo, :], T.rm[lo, 32:96], T.A1[lo, :], 0.0, Op.mult, Op.add)
+    bo = ts([pf, k5], T.bo[:], T.bi[:], odd, Op.add, 1.0 / 16, Op.mult)
+    t2 = turn([t1], T.R2[lo, :], T.R1[lo, 32:64])
+    b2 = scan([b1], T.B1[lo, :], T.rm[lo, 32:96], T.A1[lo, :], 0.0, Op.mult, Op.add)
     for h in (lo, hi):
-        zz = tt([z0, jz], T.zz[h, :], T.z0[lo, :], T.tjz[lo, :], Op.mult)
+        t3 = act([t2], T.js[h, :], T.R2[lo, 0:16], accum_out=T.dg[h, TOT:TOT + 1])
+    z0 = ts([a1], T.z0[lo, :], T.T1[lo, 4:32], 0.0, Op.is_equal)
+    ro = ts([pr], T.ro[:], quarter, 1 / 32, Op.mult, T.pr[:, 0:1], Op.add)
+    b3 = turn([b2], T.Z1[lo, :], T.B1[lo, :])
+    zz = tt([z0, j0, fj], T.zz[lo, :], T.z0[lo, :], T.tj[lo, :], Op.mult)
+    m0 = ts([p2, k4], T.mask[:, 0:64], T.kr[:, 1:65], T.pr[:, 2:3], Op.is_equal, BIG, Op.mult)
+    ee = scan([b3, fz], T.zf[lo, 1:28], T.rm[lo, 1:28], T.Z1[lo, 36:63], 0.0, Op.mult, Op.add)
+    uu = tt([b3, zz], T.uu[lo, :], T.Z1[lo, 4:32], T.zz[lo, :], Op.add)
+    qx = own(T.raw, T.raws, 0)
     for h in (lo, hi):
-        b3 = turn([b2], T.Z1[h, :], T.B1[lo, :])
-    to = sorted((d for d in range(N) if d != r and r in summed(d)), key=lambda d: not part(d))
-    m64 = ts([k3, pq], T.m64[:], T.ir[:, 0:64], T.pq[:], Op.is_equal, BIG, Op.mult)
-    ee = scan([b3, fz], ee_(1, 27), T.rm[:, 3:29], T.Z1[:, 32:58], 0.0, Op.mult, Op.add)
-    uu = tt([b3, zz], T.uu[:], T.Z1[:, 0:26], T.zz[:], Op.add)
+        sx = tt([uu, ee], T.sx[h, :], T.uu[lo, :], T.zf[lo, 0:28], Op.add)
+    ma = me[r][0]
     if z is not None:
-        qx = own(T.raw[:], T.raws[:])
-    sx = tt([uu, ee], T.sx[:], T.uu[:], ee_(0, 26), Op.add)
-    f2 = act([ee], T.f2[:], ee_(26, 27), Act.Relu, bias=-float(H))
-    rf = act([sx, ro], T.rf[:], T.sx[:].indirect(T.ro[:]))
-    bb = act([sx, bo], T.bb[:], T.sx[:].indirect(T.bo[:]))
-    rf = act([rf], T.rf[:, K:K + 1], ee_(12, 13))
-    if r >= half:
-        act([ee], slot(r, r), ee_(12, 13))
-    act([ee], T.dg[:, C:C + 1], ee_(12, 13))
-    n2 = act([f2], T.dg[:, C + 1:C + 2], T.f2[:], scale=-2.0)
-    ml = tc([mk], T.mask[:, 256:PL], T.mask[:, 0:PL - 256])
-    sxu = tc([sx], T.su[:], T.sx[:, 14:26])
-    fp = act([ml], T.pw[:, P * r:P * r + PL], T.mask[:], Act.Identity, scale=0.0, bias=BIG)
-    for s in order:
-        if s not in (lo2, z):
-            vv = act([ip, iw], vals(s), T.iw[:] if me[s][1] == C else T.ip[:], Act.Identity, bias=2.0 * me[s][0])
-    if z is not None:
-        vv = act([ip], T.vy[:], T.ip[:], Act.Identity, bias=2.0 * me[z][0] - (C - H))
-    if z is None:
-        qx = own(T.raw[:], T.raws[:])
-    ks = tc([sxu, kr], T.kr[:].indirect(T.su[:]), T.ir[:])
-    er = turn([bb], T.er[:, 0:C], T.bb[:])
-    kd = diag([ks, mk], T.kd[:], T.mask[:, 0:C], T.kr[:, 1:C + 1])
-    if hi2 is not None:
-        l2 = ts([f2, j0], T.l2[:, 0:7], T.tj[:, 0:7], T.f2[:], Op.add)
-    ke = tc([kd], T.ke[:], T.kd[:, 15:C:16])
-    kl = ts([kd], T.kl[:], T.kd[:, 15:C:16], C - 1.0, Op.min)
+        down = own(T.win, T.wins, ma, 0, 128)
+    su = tc([sx], T.su[:], T.sx[:, 0:12])
+    mk = act([m0], T.mask[:, 64:128], T.mask[:, 0:64])
+    ep = act([k3], T.er[:, C:C + Q], T.ir[:, 0:Q], bias=float(TR + C * r))
+    mk = act([mk], T.mask[:, 128:256], T.mask[:, 0:128])
+    rf = act([sx, ro], T.dg[:, TOT + 1:TOT + 17], T.sx[:, 16:28].indirect(T.ro[:]))
+    bb = act([sx, bo], T.bb[:], T.sx[:, 16:28].indirect(T.bo[:]))
+    ip = act([k6], T.ip[:], T.iq[:], bias=quarter)
+    n2 = act([sx], T.dg[:, TOT - 4:TOT - 3], nw, scale=-2.0, bias=2.0 * H)
+    ml = act([mk], T.mask[:, 256:PL], T.mask[:, 0:PL - 256])
 
+    calls = {
+        "total": ([t3], [(to, inner(r) if to == [pt] and z is not None else E, "atot", tot, [slot(r, d) for d in to])] if to else []),
+        "late total": ([t3], [([d], inner(r), "atp", tot, [T.tp[:]]) for d in part(r) if d not in to]),
+        "all codes": ([qx], [([d], way(d), "acd", codes(T.raw[:]), [codes(T.win[:, at[d]:at[d] + C])]) for d in fl]),
+        "all scales": ([qx], [([d], way(d), "asd", T.raws[:], [T.wins[:, at[d]:at[d] + C]]) for d in fl]),
+        "all table": ([rf], [([d], way(d), "art", T.dg[:, TOT:TOT + K + 1], [table(r, d, -1, K)]) for d in fl]),
+    }
+    for k in ORDER[z is not None][0]:
+        fused(*calls[k])
+    for s in order:
+        if s != lo2:
+            vc = act([ip], vals(s), T.ip[:], bias=2.0 * me[s][0] - (C - H if s == z else 0))
+
+    if z is not None:
+        quant(0)
+    ks = tc([su, m0, k3], T.kr[:].indirect(T.su[:]), T.ir[:])
+    er = turn([bb], T.er[:, 0:C], T.bb[:])
+    kd = diag([ks, mk], T.kd[:, 1:C + 1], T.mask[:, 0:C], T.kr[:, 1:C + 1])
+    if z is not None:
+        quant(1)
+    kl = ts([kd], T.kl[:], T.kd[:, 16:C + 1:16], C - 1.0, Op.min)
+    ke = tc([kd, ko], T.ke[:], T.kd[:, 16:C + 1].indirect(T.ko[:]))
+    if hi2 is not None:
+        l2 = ts([sx, j0], T.l2[:, 0:7], T.tj[:, 0:7], nw, Op.add, -float(H + FAR), Op.add)
     cq = pick([kl, qx], T.comp[:], T.raw[:], T.kl[:])
-    sc = act([er, ep, ke], T.sc[:], T.er[:].indirect(T.ke[:]))
+    sc = act([er, ep, ke], T.sc[:], T.er[:].indirect(T.ke[:, 0:K]))
+    if z is not None:
+        sf = act([er, kl], T.sf[:], T.er[:].indirect(T.kl[:, 0:(C - H) // 16]), bias=0.5 - P * z)
+    else:
+        cs = picks([kl, qx], T.comps[:], T.raws[:], T.kl[:])
+    for c in range(K):
+        tx = diag([sc, n2], T.dg[:, c:TOT:4], T.mask[:, 0:16], T.sc[:, 16 * c:16 * c + 16])
+    src = {}
+    if hi2 is not None:
+        q2 = pick([l2, cq], T.sel2[:], T.comp[:], T.l2[:, 0:7])
+    if z is not None:
+        cs = tc([kl, qx], T.comps[:], T.raws[:].indirect(T.kl[:]))
     sm = summed(r)
     n = len(sm)
     at0, at1, atm = T.sb[:, 0:1], T.sb[:, 1:2], T.sb[:, 2:3]
-    if z is None:
-        cs = act([kl, qx], T.comps[:], T.raws[:].indirect(T.kl[:]))
     tots = ("atot", len(E) * len([s for s in sm if s != r]))
     if n:
-        tS = act([n2, tots], T.js[:, 0:n], T.tl[:, 0:4 * n:4], Act.Identity,
-                 scale=1.0 if r < half else -1.0, bias=(shift if r < half else N * P + shift) / n, accum_out=T.S[:])
+        k = TOT + 20 * (r < half)
+        s0 = act([n2, tots], T.jt[:, 0:n], T.dg[:, k:k + 20 * n - 19:20], scale=1.0 if r < half else -1.0,
+                 bias=(-1.0 if r < half else N * P - 1.0) / n, accum_out=at0)
+    else:
+        s0 = act([n2], at0, tot, scale=0.0, bias=-1.0)
     if z is not None:
-        ac = act([tS, sc], T.jk[:], T.sc[:, 0:C - H], Act.Sign, bias=T.S[:], accum_out=acc)
-    s0 = act([tS], at0, T.S[:], Act.Identity, bias=-shift - 1.0) if n else act([f2], at0, T.f2[:], Act.Identity, scale=0.0, bias=-1.0)
-    if z is not None:
-        cs = act([kl, qx], T.comps[:], T.raws[:].indirect(T.kl[:]))
-    s1 = act([s0], at1, ee_(12, 13), Act.Identity, bias=at0)
+        ac = act([s0, sf], T.jk[:], T.sf[:], Act.Sign, bias=at0, accum_out=acc)
+    if hi2 is not None:
+        s1 = act([s0], at1, tot, bias=at0)
+    if z is None:
+        down = own(T.win, T.wins, ma)
+        quant(0)
 
     def here(s):
         if r in full(s):
@@ -303,113 +342,88 @@ def rank_program(g, core, T, topo):
     def sum_of(s):
         if s in sm:
             return slot(s, r), tots
-        return (T.tp[:], ("atp", len(inner(s)))) if s == z else (table(s, r, K, K + 1), here(s))
+        return (T.tp[:], ("atp", len(inner(s)))) if s == z else (table_sum(s, r), here(s))
 
-    def before():
-        return act([s0, sum_of(r - 1)[1]], atm, sum_of(r - 1)[0], Act.Identity, scale=-1.0, bias=at0)
-
-    early = r - 1 in sm + [z]
-    if lo2 is not None and early:
-        s2 = before()
-    for c in range(K):
-        tx = diag([sc, m64], T.dg[:, c:C:K], T.m64[:], T.sc[:, 64 * c:64 * c + 64])
-    scl = {}
+    if lo2 is not None:
+        s2 = act([s0, sum_of(r - 1)[1]], atm, sum_of(r - 1)[0], scale=-1.0, bias=at0)
+        src[lo2] = (T.comp, cq, T.comps, cs)
     if hi2 is not None:
-        q2 = pick([l2, cq], T.sel2[:], T.comp[:], T.l2[:, 0:7])
-        scl[hi2] = (T.sel2s, act([l2, cs], T.sel2s[:], T.comps[:].indirect(T.l2[:, 0:7])))
-    if lo2 is not None:
-        scl[lo2] = (T.comps, cs)
-    qw = [quant(0, 384, dw0)]
-    if z is not None:
-        le = ts([ac, j3], T.lze[:, 0:7], T.m2[:, 0:7], acc, Op.add, -0.5, Op.mult)
-    ma = me[r][0]
-    down = own(T.win[:, ma:ma + C], T.wins[:, ma:ma + C])
-    if z is not None:
-        qz = pick([le, cq], T.selz[:], T.comp[:], T.lze[:, 0:7])
-        qzs = act([le, cs], T.selzs[:], T.comps[:].indirect(T.lze[:, 0:7]))
-    if lo2 is not None:
-        if not early:
-            s2 = before()
-        vv = act([ip, here(lo2)], vals(lo2), T.ip[:], Act.Identity, bias=table(lo2, r, K + 1, K + 2))
+        src[hi2] = (T.sel2, q2, T.sel2s, picks([l2, cs], T.sel2s[:], T.comps[:], T.l2[:, 0:7]))
 
     def places(s):
         o = T.ot[:, K * order.index(s):K * order.index(s) + K]
         if s == r:
-            return ts([s0], o, T.rf[:, 0:K], at0, Op.add)
+            return ts([s0, rf], o, T.dg[:, TOT + 1:TOT + K + 1], at0, Op.add)
         if s == r + 1:
-            return ts([s1, here(s)], o, table(s, r), at1, Op.add)
+            return ts([s0, here(s)], o, table(s, r), at0, Op.add, tot, Op.add)
         if s == r + 2:
             return ts([s1, here(s), sum_of(r + 1)[1]], o, table(s, r), at1, Op.add, sum_of(r + 1)[0], Op.add)
-        return ts([s0 if s == r - 1 else s2, here(s)], o, table(s, r), at0 if s == r - 1 else atm, Op.add, table(s, r, K, K + 1), Op.subtract)
+        return ts([s0 if s == r - 1 else s2, here(s)], o, table(s, r), at0 if s == r - 1 else atm, Op.add, table_sum(s, r), Op.subtract)
 
-    ot = places(r)
-    qw.append(quant(384, 768, dw1))
+    if z is not None:
+        le = ts([ac, j3], T.lze[:, 0:7], T.m2[:], acc, Op.add, -0.5, Op.mult)
+    for s in order[:early]:
+        ot = places(s)
+    if z is not None:
+        qz = pick([le, cq], T.selz[:], T.comp[:], T.lze[:, 0:7])
+        qzs = picks([le, cs], T.selzs[:], T.comps[:], T.lze[:, 0:7])
 
-    at = {d: seg(d)[r][0] for d in seg(r)}
-    fl = full(r)
+    def spread(deps, a, b):
+        return tc(deps, T.pw[:].indirect(T.ot[:, a:b]), T.vv[:, 16 * a:16 * b])
 
-    def way(d):
-        return inner(r) if d == pt else share(r, d) if d in two(r) else E
-
-    def sem(d):
-        return "apc" if d == pt else "acd"
-
-    src = {}
+    pp = spread([ot, vc, fp], 0, K * early)
+    vv = vc
     if lo2 is not None:
-        src[lo2] = (T.comp, cq)
-    if hi2 is not None:
-        src[hi2] = (T.sel2, q2)
+        vv = act([vc, here(lo2)], vals(lo2), T.ip[:], bias=table(lo2, r, -1, 0))
     if z is not None:
-        src[z] = (T.selz, qz)
-        scl[z] = (T.selzs, qzs)
+        vv = act([vc, ("acz", len(inner(z)))], vals(z), vals(z), bias=T.az[:])
+    else:
+        quant(1)
+    for s in order[early:]:
+        ot = places(s)
+    if z is not None:
+        down = own(T.win, T.wins, ma, C - 128, C, [down])
+    else:
+        quant(2)
+    pp = spread([pp, ot, vv], K * early, K * len(order) - (hi2 is not None))
+    quant(len(qw))
+
     far = sorted(two(r), key=lambda d: not part(d))
-    calls = {
-        "total": ([ee], [(to, inner(r) if to == [pt] and z is not None else E, "atot", ee_(12, 13), [slot(r, d) for d in to])] if to else []),
-        "late total": ([ee], [([d], inner(r), "atp", ee_(12, 13), [T.tp[:]]) for d in part(r) if d not in to]),
-        "all codes": ([qx], [([d], way(d), sem(d), codes(T.raw[:]), [codes(T.win[:, at[d]:at[d] + C])]) for d in fl]),
-        "all scales": ([qx], [([d], way(d), sem(d), T.raws[:], [T.wins[:, at[d]:at[d] + C]]) for d in fl]),
-        "all table": ([rf], [(fl, E, "art", T.rf[:, 0:K + 1], [table(r, d, 0, K + 1) for d in fl])]),
-        "table": ([tx, n2], [(far, E, "act", T.dg[:, C - K:C + 2], [table(r, d, 0, K + 2) for d in far])]
-                  + [([d], inner(r), "acp", T.dg[:, C - K:C + 2], [table(r, d, 0, K + 2)]) for d in part(r)]),
-        "shift": ([ac], [([z], inner(r), "acz", acc, [T.az[:]])]) if z is not None else None,
-        "codes": ([src[d][1] for d in src], [([d], way(d), sem(d), codes(src[d][0][:, 0:H]), [codes(T.win[:, at[d]:at[d] + H])]) for d in src]),
-        "scales": ([scl[d][1] for d in scl], [([d], way(d), sem(d), scl[d][0][:, 0:H], [T.wins[:, at[d]:at[d] + H]]) for d in scl]),
-    }
-    for k in (("total", "all codes", "all table", "late total", "table", "shift", "all scales", "codes", "scales") if z is not None else
-              ("total", "all codes", "all table", "table", "codes", "all scales", "scales")):
-        if calls[k][1]:
-            fused(*calls[k])
-
+    calls.update({
+        "table": ([tx], [(far, E, "act", T.dg[:, TOT - K - 1:TOT + 1], [table(r, d, -1, K + 1) for d in far])]
+                  + [([d], inner(r), "acp", T.dg[:, TOT - K - 1:TOT + 1], [table(r, d, -1, K + 1)]) for d in part(r)]),
+        "codes": ([src[d][1] for d in src], [([d], way(d), "acd", codes(src[d][0][:, 0:H]), [codes(T.win[:, at[d]:at[d] + H])]) for d in src]),
+        "scales": ([src[d][3] for d in src], [([d], way(d), "asd", src[d][2][:, 0:H], [T.wins[:, at[d]:at[d] + H]]) for d in src]),
+    })
     if z is not None:
-        vv = act([("acz", len(inner(z)))], vals(z), T.vy[:], Act.Identity, bias=T.az[:])
-    for s in sorted(order, key=lambda s: s in two(r)):
-        if s != r:
-            ot = places(s)
-    no = len(order)
-    pp = tc([ot, vv, fp], T.pw[:].indirect(T.ot[:, 0:K * no]), T.vv[:, 0:16 * K * no])
+        calls["shift"] = ([ac], [([z], inner(r), "acz", acc, [T.az[:]])])
+        calls["part codes"] = ([qz], [([z], inner(r), "acd", codes(T.selz[:]), [codes(T.win[:, at[z]:at[z] + H])])])
+        calls["part scales"] = ([qzs], [([z], inner(r), "asd", T.selzs[:], [T.wins[:, at[z]:at[z] + H]])])
+    for k in ORDER[z is not None][1]:
+        fused(*calls[k])
 
-    ncd = sum(2 * len(share(s, r)) for s in two(r)) + sum(2 * len(eng(s)) for s in zed(r))
-    got = [down, ("apc", 2 * len(inner(pt))), ("acd", ncd)]
+    ncd = sum(len(share(s, r)) for s in two(r)) + sum(len(eng(s)) for s in zed(r)) + len(inner(pt))
 
     m = diag([pp, ml], T.pd[:], T.mask[:], T.pw[:, P * r:P * r + PL])
+    quant(len(qw))
     back = slice(PL - 1, 14, -8)
     m = scan([m], T.mt[lo, ::-1], T.pd[lo, back], T.pd[hi, back], BIG, Op.min, Op.min)
     for k in (0, 32):
         u = tt([m], T.my[k:k + 32, :], T.mt[0:32, ::2], T.mt[32:64, ::2], Op.min)
     for k in (0, 64):
-        il = ts([u], T.il[k:k + 64, :], T.my[0:64, :], 0.5, Op.mult)
+        il = ts([u], T.il[k:k + 64, :], T.my[lo, :], 0.5, Op.mult)
+    quant(len(qw))
 
     def fin(b):
         i = slice(128 * b, 128 * b + 128)
         o = T.il[:, 8 * b:8 * b + 8]
-        dep = [il] + got
-        return [pick(dep, T.fin[:, i], T.win[:], o), act(dep, T.fins[:, i], T.wins[:].indirect(o))]
+        return [pick([il, down, ("acd", ncd)], T.fin[:, i], T.win[:], o), picks([il, down, ("asd", ncd)], T.fins[:, i], T.wins[:], o)]
 
     def mul(b, h, deps):
         k = NO * b + h
         wi = slice(128 * k, 128 * k + 128)
         i = slice(128 * b, 128 * b + 128)
-        return do("t", deps + qw, lambda: g.tensor.matmul_mx(
+        return do("t", deps + [qw[k]], lambda: g.tensor.matmul_mx(
             T.ps[:, 512 * k:512 * k + 128], T.wq[:, wi], T.ws[:, wi], T.fin[:, i], T.fins[:, i], True, True))
 
     def out(b, h, mm):
@@ -420,11 +434,13 @@ def rank_program(g, core, T, topo):
     y = []
     for b in range(NB):
         c = fin(b)
+        if len(qw) < NO * NB and b == NB - 1:
+            quant(len(qw))
         y.append([mul(b, h, c) for h in range(NO)])
-    for bs in ((0,), (1, 2)):
-        cp = [[out(b, h, y[b][h]) for h in range(NO)] for b in bs]
+    for bl in ((0,), (1, 2)):
+        cp = [[out(b, h, y[b][h]) for h in range(NO)] for b in bl]
         for h in range(NO):
-            yi = slice(P * h + 128 * bs[0], P * h + 128 * bs[-1] + 128)
+            yi = slice(P * h + 128 * bl[0], P * h + 128 * bl[-1] + 128)
             dma("s", "dy", T.y[:, yi], T.ysb[:, yi], [cp[-1][h]])
 
     need("s", [("dy", total["dy"])])

from concourse.bass import DstId, RemoteDMATransfer
from concourse.mybir import dt, AluOpType as Op, AxisListType, ActivationFunctionType as Act

C, P, NB, NO, H = 192, 384, 3, 2, 112
K = C // 64
TR = 3200
FAR = 208
PL = P + 8
BIG = float(2 ** 20)
WIN = 3 * H + 2 * C
Q = 16 * K
TOT = 63
F32, I32, U16, U8, F8, BF = "float32", "int32", "uint16", "uint8", "float8_e4m3fn_x4", "bfloat16"


def sb(n, t):
    return ("sbuf", [128, n], t)


SCRATCH = {
    "xt": sb(4 * C, BF), "wt": sb(512 * 6, BF), "wq": sb(768, F8), "ws": sb(768, U8),
    "raw": sb(C, F8), "raws": sb(C, U8), "comp": sb(C, F8), "comps": sb(C, U8),
    "sel2": sb(H, F8), "sel2s": sb(H, U8), "selz": sb(H, F8), "selzs": sb(H, U8),
    "win": sb(WIN, F8), "wins": sb(WIN, U8), "fin": sb(P, F8), "fins": sb(P, U8),
    "pi": sb(1, I32), "pa": sb(3, I32), "pf": sb(3, F32), "pr": sb(3, F32), "ro": sb(1, U16), "ko": sb(1, U16),
    "c16": sb(28, F32), "tj": sb(28, F32), "ir": sb(C, F32), "bi": sb(12, F32), "bo": sb(12, U16), "mask": sb(PL, BF), "rm": sb(96, BF),
    "iq": sb(Q, F32), "ip": sb(Q, F32), "m2": sb(7, F32), "vv": sb(5 * Q, F32),
    "tb": sb(12, I32), "T1": sb(64, BF), "A1": sb(64, BF), "B1": sb(64, BF), "Z1": sb(64, BF), "R1": sb(64, BF), "R2": sb(32, BF),
    "zf": sb(32, F32), "uu": sb(28, F32), "z0": sb(28, F32), "zz": sb(28, F32), "sx": sb(28, F32), "su": sb(12, U16),
    "kr": sb(592, BF), "kd": sb(C + 1, BF), "kl": sb(12, U16), "ke": sb(16, U16), "bb": sb(C, F32), "er": sb(C + Q, F32),
    "sc": sb(Q, F32), "dg": sb(TOT + 61, F32), "sb": sb(5, F32), "tp": sb(1, F32), "l2": sb(8, U16),
    "jk": sb(C - H, F32), "sf": sb(C - H, F32), "sg": sb(C - H, F32), "cz": sb(1, F32), "js": sb(16, F32), "jt": sb(8, F32), "lze": sb(8, U16), "acc": sb(1, F32),
    "ct": sb(32, F32), "ot": sb(16, U16), "az": sb(1, F32),
    "pw": sb(TR + 8 * (C + P), F32), "pd": sb(PL, F32), "mt": sb(48, F32), "my": sb(24, F32), "il": sb(24, U16),
    "ysb": sb(NO * P, F32), "ps": ("psum", [128, 512 * 6], F32),
}
SEMAPHORES = ["sv", "sa", "sg", "st", "dtab", "dx", "dw0", "dw1", "dy", "sent", "atot", "atp", "act", "art", "acp", "acz", "acd", "asd"]
ORDER = ((("total", "all table", "all codes"), ("table", "all scales", "codes", "scales")),
         (("total", "late total", "all codes", "all table", "all scales"), ("table", "shift", "codes", "scales", "part codes", "part scales")))


def common(topo, src, dsts):
    e = topo.engines(src, dsts[0])
    for d in dsts[1:]:
        e = [k for k in e if k in topo.engines(src, d)]
    return e


def bits(e):
    m = 0
    for k in e:
        m |= 1 << k
    return m


def rank_program(g, core, T, topo):
    r = T.rank_of(core)
    if r is None:
        return
    cores = T.cores
    N = len(cores)
    half = N // 2

    def partner(q):
        return [d for d in (q - 1, q + 1) if 0 <= d < N and topo.chip(cores[d]) == topo.chip(cores[q])][0]

    def two(q):
        return [d for d in (q - 2, q + 2) if 0 <= d < N]

    def zed(q):
        return [d for d in (q - 1, q + 1) if 0 <= d < N and d != partner(q)]

    def others(d):
        return [s for s in range(max(0, d - 2), min(N, d + 3)) if s != d]

    def part(q):
        return [d for d in (partner(q),) if len(others(d)) == 4]

    def full(q):
        return zed(q) + [d for d in (partner(q),) if d not in part(q)]

    def seg(d):
        a, o = {}, 0
        for s in range(max(0, d - 2), min(N, d + 3)):
            n = C if s == d or d in full(s) else H
            a[s] = (o, n)
            o += n
        return a

    def ranked(d):
        return sorted(seg(d), key=lambda s: (seg(d)[s][1] == H, s != d, s == d + 2, s not in part(d)))

    def eng(q):
        return common(topo, cores[q], [c for c in cores if c != cores[q]])

    def inner(q):
        return [e for e in topo.engines(cores[q], cores[partner(q)]) if e not in eng(q)]

    def share(q, d):
        e, v = eng(q), two(q)
        n = len(e) // len(v)
        return e[n * v.index(d):n * v.index(d) + n]

    def summed(d):
        return list(range(d)) if d < half else list(range(d, N))

    def slot(s, d):
        k = TOT + 20 * (summed(d).index(s) + (d < half))
        return T.dg[:, k:k + 1]

    def table(s, d, a=0, b=K):
        k = 8 * others(d).index(s) + 1
        return T.ct[:, k + a:k + b]

    def table_sum(s, d):
        return table(s, d, -1, 0) if d in full(s) else table(s, d, K, K + 1)

    pt, me, E = partner(r), seg(r), eng(r)
    lo2 = r - 2 if r - 2 >= 0 else None
    hi2 = r + 2 if r + 2 < N else None
    z = (part(r) + [None])[0]
    order = ranked(r)
    early = 2
    qs = {"v": g.vector, "a": g.scalar, "s": g.sync, "t": g.tensor, "g": g}
    home = {"v": "sv", "a": "sa", "t": "st", "g": "sg"}
    seen, total = {}, {}

    def need(q, toks):
        for sem, val in toks:
            if seen.get((q, sem), 0) < val:
                qs[q].wait_ge(T.sem[sem], val)
                seen[(q, sem)] = val

    def do(q, deps, fn, sem=None, n=1):
        need(q, deps)
        s = sem or home[q]
        fn().then_inc(T.sem[s], n)
        total[s] = total.get(s, 0) + n
        return (s, total[s])

    V, A = g.vector, g.scalar

    def dma(q, sem, out, in_, deps=()):
        return do(q, deps, lambda: qs[q].dma_start(out, in_), sem, 16)

    def dst(c):
        rid, pid, _ = topo.addr(c)
        return DstId(rid=rid, pnc=pid)

    sent = [0]

    def fused(deps, trs):
        if trs:
            need("g", deps)
            g.remote_dma_fused([RemoteDMATransfer(dst_ids=[dst(cores[d]) for d in ds], dma_engine_mask=bits(e), remote_sem=T.sem[sem],
                                                  srcs=[a], dsts=b) for ds, e, sem, a, b in trs], local_sem=T.sem.sent)
            sent[0] += sum(len(e) for ds, e, sem, a, b in trs)

    def iota(out, pattern, base):
        return do("g", (), lambda: g.iota(out, pattern, base, 0, allow_small_or_imprecise_dtypes=True))

    def tc(deps, out, in_):
        return do("v", deps, lambda: V.tensor_copy(out, in_))

    def tt(deps, out, a, b, op):
        return do("v", deps, lambda: V.tensor_tensor(out, a, b, op))

    def ts(deps, out, a, s1, op0, s2=None, op1=None):
        if op1 is None:
            return do("v", deps, lambda: V.tensor_scalar(out, a, s1, None, op0))
        return do("v", deps, lambda: V.tensor_scalar(out, a, s1, s2, op0, op1))

    def scan(deps, out, a, b, init, op0, op1):
        return do("v", deps, lambda: V.tensor_tensor_scan(out, a, b, init, op0, op1))

    def diag(deps, out, mask, row):
        return scan(deps, out, mask, row, 0.0, Op.max, Op.min)

    def turn(deps, out, in_):
        return do("v", deps, lambda: V.transpose(out, in_))

    def fill(deps, ap, c):
        return do("v", deps, lambda: V.memset(ap, c))

    def act(deps, out, in_, func=Act.Identity, **kw):
        return do("a", deps, lambda: A.activation(out, in_, func, **kw))

    def pick(deps, out, in_, o):
        return tc(deps, out.bitcast(dt.uint32), in_.bitcast(dt.uint32).indirect(o))

    def picks(deps, out, in_, o):
        return act(deps, out, in_.indirect(o), Act.Copy)

    qw = []

    def quant(k, n=1):
        i, j = 128 * k, 128 * (k + n)
        qw.extend([do("v", dw[k // NO:(k + n - 1) // NO + 1], lambda: V.quantize_mx(T.wq[:, i:j], T.ws[:, i:j], T.wt[:, 4 * i:4 * j]))] * n)

    def own(q, s, k, a=0, b=C, deps=()):
        return do("v", [dx, *deps], lambda: V.quantize_mx(q[:, k + a:k + b], s[:, k + a:k + b], T.xt[:, 4 * a:4 * b]))

    def codes(ap):
        return ap.bitcast(dt.uint8)

    def vals(s):
        k = order.index(s)
        return T.vv[:, Q * k:Q * (k + 1)]

    acc, tot, nw = T.acc[:], T.dg[:, TOT:TOT + 1], T.sx[:, 12:13]
    to = sorted((d for d in range(N) if d != r and r in summed(d)), key=lambda d: not part(d))
    lo, hi = slice(0, 64), slice(64, 128)
    at = {d: seg(d)[r][0] for d in seg(r)}
    fl = full(r)

    def way(d):
        return inner(r) if d == pt else share(r, d) if d in two(r) else E

    for k in range(4):
        dtab = dma("s" if k % 2 == 0 else "a", "dtab", T.tb[16 * k:16 * k + 16, :], T.cnt[:])
    dx = dma("s", "dx", T.xt[:], T.x[:])
    dw = [dma("s", "dw0", T.wt[:, 0:1024], T.w[:, 0:1024])] + [dma("s", "dw1", T.wt[:, 1024:3072], T.w[:, 1024:3072])] * 2

    k0 = do("g", (), lambda: g.iota(T.pi[:], [[0, 1]], 0, 1))
    k1 = iota(T.c16[:], [[TR + C * r - FAR - 32, 2], [16, 14]], FAR)
    k4 = iota(T.kr[:, 1:C + 1], [[16, K], [0, 4], [1, 16]], C)
    k5 = iota(T.bi[:], [[32, 6], [0, 2]], 0)
    k3 = iota(T.ir[:], [[1, C]], 0)
    k6 = iota(T.iq[:], [[128, K], [2, 16]], 0)
    ft = fill((), T.T1[:], 0.0)
    u = fill((), T.rm[:], 1.0)
    fz = fill((), T.zf[:, 0:1], 0.0)
    fj = fill((), T.tj[:, 12:13], 0.0)
    for k, m in enumerate((15, 16, 96)):
        v = ts([k0], T.pa[:, k:k + 1], T.pi[:], m, Op.bitwise_and)
    fr = fill([u], T.rm[:, 16:64:16], 0.0)
    pf = tc([v], T.pf[:], T.pa[:])
    row, odd, quarter = T.pf[:, 0:1], T.pf[:, 1:2], T.pf[:, 2:3]
    fp = fill((), T.pw[:, P * r:P * r + PL], BIG)
    ts([pf], T.pr[:, 0:1], row, K - 1.0, Op.min, 4.0, Op.mult)
    pr = ts([pf], T.pr[:, 1:2], row, K - 1.0, Op.min, 64.0, Op.mult)

    act([pf, k1], T.tj[:, 0:12], T.c16[:, 0:12], bias=row)
    j0 = act([pf, k1], T.tj[:, 13:28], T.c16[:, 13:28], bias=row)
    p2 = act([pf], T.pr[:, 2:3], row, bias=float(C))
    if z is not None:
        j3 = act([j0], T.m2[:], T.tj[:, 0:7], scale=-2.0, bias=2.0 * FAR - (C - H))

    a0 = tc([dtab, ft], T.T1[lo, 20:32], T.tb[lo, :])
    a1 = ts([dtab], T.T1[lo, 4:16], T.tb[lo, :], 0.0, Op.is_gt)
    ko = ts([pr], T.ko[:], quarter, 0.5, Op.mult, T.pr[:, 1:2], Op.add)
    t1 = scan([a0, fr], T.R1[lo, 20:64], T.rm[lo, 52:96], T.T1[lo, 20:64], 0.0, Op.mult, Op.add)
    b1 = turn([a1], T.A1[lo, :], T.T1[lo, :])
    bo = ts([pf, k5], T.bo[:], T.bi[:], odd, Op.add, 1.0 / 16, Op.mult)
    t2 = turn([t1], T.R2[lo, :], T.R1[lo, 32:64])
    b2 = scan([b1], T.B1[lo, :], T.rm[lo, 32:96], T.A1[lo, :], 0.0, Op.mult, Op.add)
    for h in (lo, hi):
        t3 = act([t2], T.js[h, :], T.R2[lo, 0:16], accum_out=T.dg[h, TOT:TOT + 1])
    z0 = ts([a1], T.z0[lo, :], T.T1[lo, 4:32], 0.0, Op.is_equal)
    ro = ts([pr], T.ro[:], quarter, 1 / 32, Op.mult, T.pr[:, 0:1], Op.add)
    b3 = turn([b2], T.Z1[lo, :], T.B1[lo, :])
    zz = tt([z0, j0, fj], T.zz[lo, :], T.z0[lo, :], T.tj[lo, :], Op.mult)
    m0 = ts([p2, k4], T.mask[:, 0:64], T.kr[:, 1:65], T.pr[:, 2:3], Op.is_equal, BIG, Op.mult)
    ee = scan([b3, fz], T.zf[lo, 1:28], T.rm[lo, 1:28], T.Z1[lo, 36:63], 0.0, Op.mult, Op.add)
    uu = tt([b3, zz], T.uu[lo, :], T.Z1[lo, 4:32], T.zz[lo, :], Op.add)
    qx = own(T.raw, T.raws, 0)
    for h in (lo, hi):
        sx = tt([uu, ee], T.sx[h, :], T.uu[lo, :], T.zf[lo, 0:28], Op.add)
    ma = me[r][0]
    if z is not None:
        down = own(T.win, T.wins, ma, 0, 128)
    su = tc([sx], T.su[:], T.sx[:, 0:12])
    mk = act([m0], T.mask[:, 64:128], T.mask[:, 0:64])
    ep = act([k3], T.er[:, C:C + Q], T.ir[:, 0:Q], bias=float(TR + C * r))
    mk = act([mk], T.mask[:, 128:256], T.mask[:, 0:128])
    rf = act([sx, ro], T.dg[:, TOT + 1:TOT + 17], T.sx[:, 16:28].indirect(T.ro[:]))
    bb = act([sx, bo], T.bb[:], T.sx[:, 16:28].indirect(T.bo[:]))
    ip = act([k6], T.ip[:], T.iq[:], bias=quarter)
    n2 = act([sx], T.dg[:, TOT - 4:TOT - 3], nw, scale=-2.0, bias=2.0 * H)
    ml = act([mk], T.mask[:, 256:PL], T.mask[:, 0:PL - 256])

    calls = {
        "total": ([t3], [(to, inner(r) if to == [pt] and z is not None else E, "atot", tot, [slot(r, d) for d in to])] if to else []),
        "late total": ([t3], [([d], inner(r), "atp", tot, [T.tp[:]]) for d in part(r) if d not in to]),
        "all codes": ([qx], [([d], way(d), "acd", codes(T.raw[:]), [codes(T.win[:, at[d]:at[d] + C])]) for d in fl]),
        "all scales": ([qx], [([d], way(d), "asd", T.raws[:], [T.wins[:, at[d]:at[d] + C]]) for d in fl]),
        "all table": ([rf], [([d], way(d), "art", T.dg[:, TOT:TOT + K + 1], [table(r, d, -1, K)]) for d in fl]),
    }
    for k in ORDER[z is not None][0]:
        fused(*calls[k])
    for s in order:
        if s != lo2:
            vc = act([ip], vals(s), T.ip[:], bias=2.0 * me[s][0] - (C - H if s == z else 0))

    if z is not None:
        quant(0)
    ks = tc([su, m0, k3], T.kr[:].indirect(T.su[:]), T.ir[:])
    er = turn([bb], T.er[:, 0:C], T.bb[:])
    kd = diag([ks, mk], T.kd[:, 1:C + 1], T.mask[:, 0:C], T.kr[:, 1:C + 1])
    if z is not None:
        quant(1)
    kl = ts([kd], T.kl[:], T.kd[:, 16:C + 1:16], C - 1.0, Op.min)
    ke = tc([kd, ko], T.ke[:], T.kd[:, 16:C + 1].indirect(T.ko[:]))
    if hi2 is not None:
        l2 = ts([sx, j0], T.l2[:, 0:7], T.tj[:, 0:7], nw, Op.add, -float(H + FAR), Op.add)
    cq = pick([kl, qx], T.comp[:], T.raw[:], T.kl[:])
    sc = act([er, ep, ke], T.sc[:], T.er[:].indirect(T.ke[:, 0:K]))
    if z is not None:
        sf = act([er, kl], T.sf[:], T.er[:].indirect(T.kl[:, 0:(C - H) // 16]), bias=0.5 - P * z)
    else:
        cs = picks([kl, qx], T.comps[:], T.raws[:], T.kl[:])
    for c in range(K):
        tx = diag([sc, n2], T.dg[:, c:TOT:4], T.mask[:, 0:16], T.sc[:, 16 * c:16 * c + 16])
    src = {}
    if hi2 is not None:
        q2 = pick([l2, cq], T.sel2[:], T.comp[:], T.l2[:, 0:7])
    if z is not None:
        cs = tc([kl, qx], T.comps[:], T.raws[:].indirect(T.kl[:]))
    sm = summed(r)
    n = len(sm)
    at0, at1, atm = T.sb[:, 0:1], T.sb[:, 1:2], T.sb[:, 2:3]
    tots = ("atot", len(E) * len([s for s in sm if s != r]))
    if n:
        k = TOT + 20 * (r < half)
        s0 = act([n2, tots], T.jt[:, 0:n], T.dg[:, k:k + 20 * n - 19:20], scale=1.0 if r < half else -1.0,
                 bias=(-1.0 if r < half else N * P - 1.0) / n, accum_out=at0)
    else:
        s0 = act([n2], at0, tot, scale=0.0, bias=-1.0)
    if z is not None:
        ac = act([s0, sf], T.jk[:], T.sf[:], Act.Sign, bias=at0, accum_out=acc)
    if hi2 is not None:
        s1 = act([s0], at1, tot, bias=at0)
    if z is None:
        down = own(T.win, T.wins, ma)
        quant(0)

    def here(s):
        if r in full(s):
            return ("art", sum(len(eng(q)) for q in others(r) if r in full(q)))
        return ("acp", len(inner(s))) if s == z else ("act", sum(len(eng(q)) for q in two(r)))

    def sum_of(s):
        if s in sm:
            return slot(s, r), tots
        return (T.tp[:], ("atp", len(inner(s)))) if s == z else (table_sum(s, r), here(s))

    if lo2 is not None:
        s2 = act([s0, sum_of(r - 1)[1]], atm, sum_of(r - 1)[0], scale=-1.0, bias=at0)
        src[lo2] = (T.comp, cq, T.comps, cs)
    if hi2 is not None:
        src[hi2] = (T.sel2, q2, T.sel2s, picks([l2, cs], T.sel2s[:], T.comps[:], T.l2[:, 0:7]))

    def places(s):
        o = T.ot[:, K * order.index(s):K * order.index(s) + K]
        if s == r:
            return ts([s0, rf], o, T.dg[:, TOT + 1:TOT + K + 1], at0, Op.add)
        if s == r + 1:
            return ts([s0, here(s)], o, table(s, r), at0, Op.add, tot, Op.add)
        if s == r + 2:
            return ts([s1, here(s), sum_of(r + 1)[1]], o, table(s, r), at1, Op.add, sum_of(r + 1)[0], Op.add)
        return ts([s0 if s == r - 1 else s2, here(s)], o, table(s, r), at0 if s == r - 1 else atm, Op.add, table_sum(s, r), Op.subtract)

    if z is not None:
        le = ts([ac, j3], T.lze[:, 0:7], T.m2[:], acc, Op.add, -0.5, Op.mult)
    for s in order[:early]:
        ot = places(s)
    if z is not None:
        qz = pick([le, cq], T.selz[:], T.comp[:], T.lze[:, 0:7])
        qzs = picks([le, cs], T.selzs[:], T.comps[:], T.lze[:, 0:7])

    def spread(deps, a, b):
        return tc(deps, T.pw[:].indirect(T.ot[:, a:b]), T.vv[:, 16 * a:16 * b])

    pp = spread([ot, vc, fp], 0, K * early)
    vv = vc
    if lo2 is not None:
        vv = act([vc, here(lo2)], vals(lo2), T.ip[:], bias=table(lo2, r, -1, 0))
    if z is not None:
        vv = act([vc, ("acz", len(inner(z)))], vals(z), vals(z), bias=T.az[:])
    else:
        quant(1)
    for s in order[early:]:
        ot = places(s)
    if z is not None:
        down = own(T.win, T.wins, ma, C - 128, C, [down])
    else:
        quant(2)
    pp = spread([pp, ot, vv], K * early, K * len(order) - (hi2 is not None))
    quant(len(qw))

    far = sorted(two(r), key=lambda d: not part(d))
    calls.update({
        "table": ([tx], [(far, E, "act", T.dg[:, TOT - K - 1:TOT + 1], [table(r, d, -1, K + 1) for d in far])]
                  + [([d], inner(r), "acp", T.dg[:, TOT - K - 1:TOT + 1], [table(r, d, -1, K + 1)]) for d in part(r)]),
        "codes": ([src[d][1] for d in src], [([d], way(d), "acd", codes(src[d][0][:, 0:H]), [codes(T.win[:, at[d]:at[d] + H])]) for d in src]),
        "scales": ([src[d][3] for d in src], [([d], way(d), "asd", src[d][2][:, 0:H], [T.wins[:, at[d]:at[d] + H]]) for d in src]),
    })
    if z is not None:
        calls["shift"] = ([ac], [([z], inner(r), "acz", acc, [T.az[:]])])
        calls["part codes"] = ([qz], [([z], inner(r), "acd", codes(T.selz[:]), [codes(T.win[:, at[z]:at[z] + H])])])
        calls["part scales"] = ([qzs], [([z], inner(r), "asd", T.selzs[:], [T.wins[:, at[z]:at[z] + H]])])
    for k in ORDER[z is not None][1]:
        fused(*calls[k])

    ncd = sum(len(share(s, r)) for s in two(r)) + sum(len(eng(s)) for s in zed(r)) + len(inner(pt))

    m = diag([pp, ml], T.pd[:], T.mask[:], T.pw[:, P * r:P * r + PL])
    quant(len(qw))
    back = slice(PL - 1, 14, -8)
    m = scan([m], T.mt[lo, ::-1], T.pd[lo, back], T.pd[hi, back], BIG, Op.min, Op.min)
    for k in (0, 32):
        u = tt([m], T.my[k:k + 32, :], T.mt[0:32, ::2], T.mt[32:64, ::2], Op.min)
    for k in (0, 64):
        il = ts([u], T.il[k:k + 64, :], T.my[lo, :], 0.5, Op.mult)
    quant(len(qw))

    def fin(b):
        i = slice(128 * b, 128 * b + 128)
        o = T.il[:, 8 * b:8 * b + 8]
        return [pick([il, down, ("acd", ncd)], T.fin[:, i], T.win[:], o), picks([il, down, ("asd", ncd)], T.fins[:, i], T.wins[:], o)]

    def mul(b, h, deps):
        k = NO * b + h
        wi = slice(128 * k, 128 * k + 128)
        i = slice(128 * b, 128 * b + 128)
        return do("t", deps + [qw[k]], lambda: g.tensor.matmul_mx(
            T.ps[:, 512 * k:512 * k + 128], T.wq[:, wi], T.ws[:, wi], T.fin[:, i], T.fins[:, i], True, True))

    def out(b, h, mm):
        k = NO * b + h
        yi = slice(P * h + 128 * b, P * h + 128 * b + 128)
        return (tc if h == 0 else act)([mm], T.ysb[:, yi], T.ps[:, 512 * k:512 * k + 128])

    y = []
    for b in range(NB):
        c = fin(b)
        if len(qw) < NO * NB and b == NB - 1:
            quant(len(qw))
        y.append([mul(b, h, c) for h in range(NO)])
    for bl in ((0,), (1, 2)):
        cp = [[out(b, h, y[b][h]) for h in range(NO)] for b in bl]
        for h in range(NO):
            yi = slice(P * h + 128 * bl[0], P * h + 128 * bl[-1] + 128)
            dma("s", "dy", T.y[:, yi], T.ysb[:, yi], [cp[-1][h]])

    need("s", [("dy", total["dy"])])
    g.wait_ge(T.sem.sent, sent[0])
    need("g", [(s, total[s]) for s in total if s != "dy"])
